import numpy as np
import ml_dtypes


def mxq(x, axis, fmt="e4m3"):
    dtype, down = {"e4m3": (ml_dtypes.float8_e4m3fn, 7), "e5m2": (ml_dtypes.float8_e5m2, 14)}[fmt]
    v = np.moveaxis(np.asarray(x, np.float32).astype(ml_dtypes.bfloat16).astype(np.float64), axis, -1)
    blocks = v.reshape(v.shape[:-1] + (-1, 32))
    amax = np.abs(blocks).max(-1, keepdims=True)
    byte = np.maximum(np.where(amax > 0, np.frexp(amax)[1] - 1 + 127, 0) - down, 1)
    scale = np.exp2(byte - 127.0)
    codes = (blocks / scale).astype(np.float32).astype(dtype).astype(np.float64)
    return np.moveaxis((codes * scale).reshape(v.shape), -1, axis)


WIDE = False


def mx_kscale(k):
    if not WIDE:
        return np.ones(k)
    levels = np.array([10, -10, 5, -5, 0])
    if k % 512:
        return np.exp2(np.random.permutation(np.resize(levels, k // 32))).repeat(32)
    a = np.empty((k // 512, 16))
    for p in range(k // 512):
        a[p, :8] = np.random.permutation(np.resize(levels, 8))
        for g in range(8):
            far = levels[np.abs(levels - a[p, g]) >= 10]
            a[p, g + 8] = far[np.random.randint(len(far))]
    return np.exp2(a.ravel()).repeat(32)


def f64(x):
    return np.asarray(x).astype(np.float64)


def striped(idx):
    return np.tile(idx.reshape(-1, 16).T, (8, 1)).astype(np.uint16)


def unstriped(offs):
    return offs[:16].T.reshape(-1).astype(np.int64)


def striped8(idx):
    return np.concatenate([x.reshape(-1, 16).T for x in idx]).astype(np.uint16)


def runs(offs, k):
    lists = np.stack([offs[16 * r : 16 * r + 16].T.reshape(-1) for r in range(8)]).astype(np.int64)
    return lists[np.arange(k) % 512 // 64]


def pack_weight(w):
    k, n = w.shape
    w = f64(np.asarray(w, np.float32).astype(ml_dtypes.bfloat16)).reshape(k // 32, 32, n)
    amax = np.abs(w).max(1)
    byte = np.clip(np.where(amax > 0, np.frexp(amax)[1] - 1 + 127 - 7, 1), 1, 254)
    scaled = (w * np.exp2(127.0 - byte)[:, None, :]).reshape(k, n).astype(np.float32)
    words = np.ascontiguousarray(scaled.reshape(k // 512, 128, 4, n).transpose(0, 1, 3, 2)).astype(ml_dtypes.float8_e4m3fn).view(np.uint8)
    return words, np.ascontiguousarray(byte.astype(np.uint8).reshape(k // 512, 16, n))


def unpack_weight(words, scales):
    g, p, n, _ = words.shape
    vals = np.ascontiguousarray(words).view(ml_dtypes.float8_e4m3fn).astype(np.float64) * np.repeat(np.exp2(scales.astype(np.float64) - 127.0), 8, axis=1)[..., None]
    return vals.transpose(0, 1, 3, 2).reshape(g * 512, n)


E2M1 = np.array([0.0, 0.5, 1.0, 1.5, 2.0, 3.0, 4.0, 6.0, -0.0, -0.5, -1.0, -1.5, -2.0, -3.0, -4.0, -6.0])


def pack_fp4(w):
    k, n = w.shape
    w = f64(np.asarray(w, np.float32).astype(ml_dtypes.bfloat16)).reshape(k // 32, 32, n)
    amax = np.abs(w).max(1)
    mant, ex = np.frexp(amax / 6.0)
    byte = np.clip(np.where(amax > 0, np.where(mant > 0.5, ex, ex - 1) + 127, 1), 1, 254)
    scaled = (w * np.exp2(127.0 - byte)[:, None, :]).reshape(k, n).astype(np.float32)
    c = np.ascontiguousarray(scaled.reshape(k // 512, 128, 4, n).transpose(0, 1, 3, 2)).astype(ml_dtypes.float4_e2m1fn).view(np.uint8) & 0xF
    words = (c[..., 0::2] | (c[..., 1::2] << 4)).reshape(k // 512, 128, 2 * n)
    return np.ascontiguousarray(words), np.ascontiguousarray(byte.astype(np.uint8).reshape(k // 512, 16, n))


def unpack_fp4(words, scales):
    g, _, n = scales.shape
    words = np.ascontiguousarray(words).reshape(g, 128, n, 2)
    nib = np.empty((g, 128, n, 4), np.uint8)
    nib[..., 0::2] = words & 0xF
    nib[..., 1::2] = words >> 4
    vals = E2M1[nib] * np.repeat(np.exp2(scales.astype(np.float64) - 127.0), 8, axis=1)[..., None]
    return vals.transpose(0, 1, 3, 2).reshape(g * 512, n)


def relu(v):
    return np.maximum(v, 0.0)

def planes(y):
    n, m = y.shape
    v = y.astype(np.float32).astype(ml_dtypes.bfloat16).astype(np.float64).reshape(n // 32, 32, m)
    top = np.abs(v).max(1)
    byte = np.clip(np.where(top > 0, np.frexp(top)[1] - 1 + 127 - 7, 1), 1, 254)
    codes = (v * np.exp2(127.0 - byte)[:, None, :]).reshape(n, m).astype(np.float32).astype(ml_dtypes.float8_e4m3fn).view(np.uint8)
    words = codes.reshape(n // 512, 128, 4, m).transpose(0, 1, 3, 2)
    return np.ascontiguousarray(words), np.ascontiguousarray(byte.astype(np.uint8).reshape(n // 512, 16, m))


K, T, S, V, N, H = 512, 2048, 512, 256, 512, 512


def setup_inputs():
    n = np.random.standard_normal
    s = mx_kscale(K)[:, None]
    u = mx_kscale(H)
    packed_xT = pack_weight(n((K, T)) * s)
    packed_w2 = pack_fp4(n((H, N)) / np.sqrt(H) / u[:, None])
    return {
        "x_words": packed_xT[0],
        "x_scales": packed_xT[1],
        "w1": (n((K, H)) / np.sqrt(K) / s * u).astype(np.float32),
        "t1": (0.5 * n((H, V)) * u[:, None]).astype(np.float32),
        "t2": (0.5 * n((H, V)) * u[:, None]).astype(np.float32),
        "t3": (0.5 * n((H, V)) * u[:, None]).astype(np.float32),
        "w2_words": packed_w2[0],
        "w2_scales": packed_w2[1],
        "offs": striped(np.random.permutation(T)[:S]),
        "p1": striped8(np.stack([np.random.permutation(S)[:V] for _ in range(8)])),
        "p2": striped8(np.stack([np.random.permutation(S)[:V] for _ in range(8)])),
        "p3": striped8(np.stack([np.random.permutation(S)[:V] for _ in range(8)])),
    }


def reference(x_words, x_scales, w1, t1, t2, t3, w2_words, w2_scales, offs, p1, p2, p3):
    xq = unpack_weight(x_words, x_scales)[:, unstriped(offs)]
    y = mxq(f64(w1), 0, "e4m3").T @ xq
    z = relu(np.maximum(np.maximum(y[np.arange(H)[:, None], runs(p1, H)] + f64(t1), y[np.arange(H)[:, None], runs(p2, H)] + f64(t2)), y[np.arange(H)[:, None], runs(p3, H)] + f64(t3)))
    out_0 = unpack_fp4(w2_words, w2_scales).T @ mxq(z, 0, "e4m3")
    return (out_0,) + planes(out_0)

@@ -1,0 +1,151 @@
+from contextlib import ExitStack
+
+import concourse.mybir as mybir
+
+F32 = mybir.dt.float32
+BF16 = mybir.dt.bfloat16
+I32 = mybir.dt.int32
+U32 = mybir.dt.uint32
+U16 = mybir.dt.uint16
+U8 = mybir.dt.uint8
+FP8X4 = mybir.dt.float8_e4m3fn_x4
+FP4X4 = mybir.dt.float4_e2m1fn_x4
+ALU = mybir.AluOpType
+ACT = mybir.ActivationFunctionType
+
+P = 128
+PACK = 4
+K, T, S, V, N, H = 512, 2048, 512, 256, 512, 512
+HALF_S = S // 2
+HALF_V = V // 2
+FLOPS = 2 * K * H * S + 2 * H * N * V
+
+
+def weave_src(ap):
+    return ap.rearrange("p t (c i) -> p c t i", i=4)
+
+
+def weave_dst(ap):
+    return ap.rearrange("p (c i t) -> p c t i", i=4, t=PACK)
+
+
+def tile_picked_tropic_relu_po_kernel(
+    tc, x_words, x_scales, w1, t1, t2, t3, w2_words, w2_scales, offs, p1, p2, p3, out_0, out_1, out_2
+):
+    nc = tc.nc
+    with ExitStack() as ctx:
+        sb = ctx.enter_context(tc.tile_pool(name="sb", bufs=1))
+        reuse = ctx.enter_context(tc.tile_pool(name="reuse", bufs=1))
+        ps = ctx.enter_context(tc.psum_pool(name="ps", bufs=1))
+
+        def tile(name, shape, dtype):
+            return sb.tile(shape, dtype, name=name, align_bytes=64)
+
+        offs_t = tile("offs_t", [P, S // 16], U16)
+        p_t = [tile("p_t%d" % l, [P, V // 16], U16) for l in range(3)]
+        xs_raw = sb.tile([P, T], U8, name="xs_raw", tag="slot", align_bytes=64)
+        xw_raw = tile("xw_raw", [P, T], U32)
+        w1_raw = reuse.tile([P, PACK, H], F32, name="w1_raw", offset=4032, align_bytes=64)
+        w2s_raw = tile("w2s_raw", [P, N], U8)
+
+        nc.vector.memset(xs_raw[:].bitcast(I32), 0)
+        nc.gpsimd.memset(w2s_raw[:].bitcast(I32), 0)
+
+        nc.sync.dma_start(w1_raw[:], w1.rearrange("(p j) c -> p j c", j=PACK))
+        nc.sync.dma_start(offs_t[:], offs)
+        for l, p in enumerate((p1, p2, p3)):
+            nc.sync.dma_start(p_t[l][:], p)
+        nc.sync.dma_start(xw_raw[:].bitcast(I32), x_words[0].rearrange("p n t -> p (n t)").bitcast(I32))
+        for q in range(4):
+            eng = nc.scalar if q < 2 else nc.gpsimd
+            eng.dma_start(xs_raw[32 * q : 32 * q + 4, :].bitcast(I32), x_scales[0, 4 * q : 4 * q + 4, :].bitcast(I32))
+        for q in range(4):
+            nc.gpsimd.dma_start(w2s_raw[32 * q : 32 * q + 4, :].bitcast(I32), w2_scales[0, 4 * q : 4 * q + 4, :].bitcast(I32))
+
+        xs = tile("xs", [P, S], U8)
+        nc.vector.tensor_copy(xs[:], xs_raw[:].indirect(offs_t[:]))
+
+        w1_bf = tile("w1_bf", [P, PACK * H], BF16)
+        src = w1_raw[:].rearrange("p j (m t) -> p m j t", t=PACK)
+        dst = w1_bf[:].rearrange("p (t m j) -> p m j t", t=PACK, j=PACK)
+        nc.scalar.copy(dst[:, :48], src[:, :48])
+        nc.vector.tensor_copy(dst[:, 48:], src[:, 48:])
+        w2w_raw = reuse.tile([P, 2 * N], U8, name="w2w_raw", offset=4096, align_bytes=64)
+        steps = [reuse.tile([P, PACK, V], F32, name="step%d" % l, offset=off, align_bytes=64)
+                 for l, off in enumerate((0, 5120, 9216))]
+        nc.sync.dma_start(w2w_raw[:].bitcast(I32), w2_words[0].bitcast(I32))
+        for l, tt in enumerate((t1, t2, t3)):
+            nc.sync.dma_start(steps[l][:], tt.rearrange("(p t) v -> p t v", t=PACK))
+        w1w = tile("w1w", [P, H], U32)
+        w1s = tile("w1s", [P, H], U8)
+        nc.vector.quantize_mx(w1w[:].bitcast(FP8X4), w1s[:], w1_bf[:])
+
+        xw = sb.tile([P, S], U32, name="xw", tag="slot", align_bytes=64)
+        y = [tile("y%d" % t, [P, S], F32) for t in range(PACK)]
+        for h in range(2):
+            cols = slice(h * HALF_S, (h + 1) * HALF_S)
+            nc.vector.tensor_copy(xw[:, cols], xw_raw[:].indirect(offs_t[:, h * 16 : (h + 1) * 16]))
+            acc = ps.tile([P, HALF_S], F32, name="acc_first%d" % h)
+            nc.tensor.matmul_mx(acc[:], lhsT=w1w[:, :P].bitcast(FP8X4), lhsT_scale=w1s[:, :P],
+                                rhs=xw[:, cols].bitcast(FP8X4), rhs_scale=xs[:, cols], start=True, stop=True)
+            nc.scalar.copy(y[0][:, cols], acc[:])
+        for t in range(1, PACK):
+            m = slice(t * P, (t + 1) * P)
+            acc = ps.tile([P, S], F32, name="acc%d" % t)
+            nc.tensor.matmul_mx(acc[:], lhsT=w1w[:, m].bitcast(FP8X4), lhsT_scale=w1s[:, m],
+                                rhs=xw[:].bitcast(FP8X4), rhs_scale=xs[:], start=True, stop=True)
+            nc.scalar.copy(y[t][:], acc[:])
+
+        w2w = tile("w2w", [P, 2 * N], U8)
+        w2s = tile("w2s", [P, N], U8)
+        nc.vector.tensor_copy(w2w[:].rearrange("p (t m b) -> p m t b", t=PACK, b=2),
+                              w2w_raw[:].rearrange("p (m t b) -> p m t b", t=PACK, b=2))
+        nc.vector.tensor_copy(w2s[:].rearrange("p (t m) -> p m t", t=PACK),
+                              w2s_raw[:].rearrange("p (m t) -> p m t", t=PACK))
+
+        cand = []
+        for l in range(2):
+            a = tile("a%d" % l, [P, PACK, V], F32)
+            for t in range(PACK):
+                nc.vector.tensor_tensor(a[:, t, :], y[t][:].indirect(p_t[l][:]), steps[l][:, t, :], ALU.add)
+            b = tile("b%d" % l, [P, PACK * V], BF16)
+            nc.scalar.activation(weave_dst(b[:]), weave_src(a[:]), ACT.Relu)
+            cand.append(b)
+        best2 = tile("best2", [P, PACK * V], BF16)
+        nc.vector.tensor_tensor(best2[:], cand[0][:], cand[1][:], ALU.max)
+
+        ow = tile("ow", [P, V], U32)
+        osc = tile("osc", [P, V], U8)
+        out_rows = out_0.rearrange("(p t) v -> p t v", t=PACK)
+        out_words = out_1[0].rearrange("p v b -> p (v b)").bitcast(I32)
+        for h in range(2):
+            vs = slice(h * HALF_V, (h + 1) * HALF_V)
+            zs = slice(h * PACK * HALF_V, (h + 1) * PACK * HALF_V)
+            a = tile("a2_%d" % h, [P, PACK, HALF_V], F32)
+            for t in range(PACK):
+                nc.vector.tensor_tensor(a[:, t, :], y[t][:].indirect(p_t[2][:, h * 8 : (h + 1) * 8]), steps[2][:, t, vs], ALU.add)
+            z = tile("z%d" % h, [P, PACK * HALF_V], BF16)
+            if h == 0:
+                b = tile("b2", [P, PACK * HALF_V], BF16)
+                nc.scalar.copy(weave_dst(b[:]), weave_src(a[:]))
+                nc.vector.tensor_tensor(z[:], b[:], best2[:, zs], ALU.max)
+            else:
+                nc.vector.tensor_tensor(weave_dst(z[:]), weave_src(a[:]), weave_dst(best2[:, zs]), ALU.max)
+            zw = tile("zw%d" % h, [P, HALF_V], U32)
+            zsc = tile("zsc%d" % h, [P, HALF_V], U8)
+            nc.vector.quantize_mx(zw[:].bitcast(FP8X4), zsc[:], z[:])
+            acc = ps.tile([P, PACK, HALF_V], F32, name="acc_out%d" % h)
+            for t in range(PACK):
+                nc.tensor.matmul_mx(acc[:, t, :], lhsT=w2w[:, 2 * P * t : 2 * P * (t + 1)].bitcast(FP4X4),
+                                    lhsT_scale=w2s[:, P * t : P * (t + 1)],
+                                    rhs=zw[:].bitcast(FP8X4), rhs_scale=zsc[:], start=True, stop=True)
+            o = tile("o%d" % h, [P, PACK, HALF_V], F32)
+            nc.scalar.copy(o[:], acc[:])
+            nc.sync.dma_start(out_rows[:, :, vs], o[:])
+            ob = tile("ob%d" % h, [P, PACK * HALF_V], BF16)
+            nc.vector.tensor_copy(weave_dst(ob[:]), weave_src(o[:]))
+            nc.vector.quantize_mx(ow[:, vs].bitcast(FP8X4), osc[:, vs], ob[:])
+            nc.sync.dma_start(out_words[:, vs], ow[:, vs].bitcast(I32))
+        for q in range(4):
+            eng = nc.sync if q < 2 else nc.scalar
+            eng.dma_start(out_2[0, 4 * q : 4 * q + 4, :].bitcast(I32), osc[32 * q : 32 * q + 4, :].bitcast(I32))

@@ -43,44 +43,47 @@ def tile_picked_tropic_relu_po_kernel(
 
         offs_t = tile("offs_t", [P, S // 16], U16)
         p_t = [tile("p_t%d" % l, [P, V // 16], U16) for l in range(3)]
-        xs_raw = sb.tile([P, T], U8, name="xs_raw", tag="slot", align_bytes=64)
+        xs_raw = reuse.tile([P, T], U8, name="xs_raw", offset=4032, align_bytes=64)
         xw_raw = tile("xw_raw", [P, T], U32)
-        w1_raw = reuse.tile([P, PACK, H], F32, name="w1_raw", offset=4032, align_bytes=64)
-        w2s_raw = tile("w2s_raw", [P, N], U8)
+        w1_raw = reuse.tile([P, PACK, H], F32, name="w1_raw", offset=9728, align_bytes=64)
 
         nc.vector.memset(xs_raw[:].bitcast(I32), 0)
-        nc.gpsimd.memset(w2s_raw[:].bitcast(I32), 0)
 
-        nc.sync.dma_start(w1_raw[:], w1.rearrange("(p j) c -> p j c", j=PACK))
         nc.sync.dma_start(offs_t[:], offs)
-        for l, p in enumerate((p1, p2, p3)):
-            nc.sync.dma_start(p_t[l][:], p)
+        nc.sync.dma_start(p_t[0][:], p1)
+        nc.sync.dma_start(w1_raw[:], w1.rearrange("(p j) c -> p j c", j=PACK))
+        nc.sync.dma_start(p_t[1][:], p2)
         nc.sync.dma_start(xw_raw[:].bitcast(I32), x_words[0].rearrange("p n t -> p (n t)").bitcast(I32))
+        nc.sync.dma_start(p_t[2][:], p3)
         for q in range(4):
-            eng = nc.scalar if q < 2 else nc.gpsimd
-            eng.dma_start(xs_raw[32 * q : 32 * q + 4, :].bitcast(I32), x_scales[0, 4 * q : 4 * q + 4, :].bitcast(I32))
-        for q in range(4):
-            nc.gpsimd.dma_start(w2s_raw[32 * q : 32 * q + 4, :].bitcast(I32), w2_scales[0, 4 * q : 4 * q + 4, :].bitcast(I32))
+            nc.scalar.dma_start(xs_raw[32 * q : 32 * q + 4, :].bitcast(I32), x_scales[0, 4 * q : 4 * q + 4, :].bitcast(I32))
 
         xs = tile("xs", [P, S], U8)
         nc.vector.tensor_copy(xs[:], xs_raw[:].indirect(offs_t[:]))
 
-        w1_bf = tile("w1_bf", [P, PACK * H], BF16)
-        src = w1_raw[:].rearrange("p j (m t) -> p m j t", t=PACK)
-        dst = w1_bf[:].rearrange("p (t m j) -> p m j t", t=PACK, j=PACK)
-        nc.scalar.copy(dst[:, :48], src[:, :48])
-        nc.vector.tensor_copy(dst[:, 48:], src[:, 48:])
+        src = w1_raw[:].rearrange("p j (m u e) -> p u m j e", u=2, e=2)
+        w1w = tile("w1w", [P, H], U32)
+        w1s = tile("w1s", [P, H], U8)
+        w1_bf = [tile("w1_bf%d" % u, [P, 2 * H], BF16) for u in range(2)]
+        dst = [w[:].rearrange("p (e m j) -> p m j e", e=2, j=PACK) for w in w1_bf]
+        nc.scalar.copy(dst[0], src[:, 0])
+        nc.vector.tensor_copy(dst[1], src[:, 1])
+        for u in (1, 0):
+            cols = slice(2 * P * u, 2 * P * (u + 1))
+            nc.vector.quantize_mx(w1w[:, cols].bitcast(FP8X4), w1s[:, cols], w1_bf[u][:])
+
         w2w_raw = reuse.tile([P, 2 * N], U8, name="w2w_raw", offset=4096, align_bytes=64)
+        w2s_raw = reuse.tile([P, N], U8, name="w2s_raw", offset=5120, align_bytes=64)
         steps = [reuse.tile([P, PACK, V], F32, name="step%d" % l, offset=off, align_bytes=64)
-                 for l, off in enumerate((0, 5120, 9216))]
+                 for l, off in enumerate((0, 5632, 9728))]
+        nc.vector.memset(w2s_raw[:].bitcast(I32), 0)
         nc.sync.dma_start(w2w_raw[:].bitcast(I32), w2_words[0].bitcast(I32))
         for l, tt in enumerate((t1, t2, t3)):
             nc.sync.dma_start(steps[l][:], tt.rearrange("(p t) v -> p t v", t=PACK))
-        w1w = tile("w1w", [P, H], U32)
-        w1s = tile("w1s", [P, H], U8)
-        nc.vector.quantize_mx(w1w[:].bitcast(FP8X4), w1s[:], w1_bf[:])
+        for q in range(4):
+            nc.sync.dma_start(w2s_raw[32 * q : 32 * q + 4, :].bitcast(I32), w2_scales[0, 4 * q : 4 * q + 4, :].bitcast(I32))
 
-        xw = sb.tile([P, S], U32, name="xw", tag="slot", align_bytes=64)
+        xw = tile("xw", [P, S], U32)
         y = [tile("y%d" % t, [P, S], F32) for t in range(PACK)]
         for h in range(2):
             cols = slice(h * HALF_S, (h + 1) * HALF_S)
@@ -134,13 +137,15 @@ def tile_picked_tropic_relu_po_kernel(
             zw = tile("zw%d" % h, [P, HALF_V], U32)
             zsc = tile("zsc%d" % h, [P, HALF_V], U8)
             nc.vector.quantize_mx(zw[:].bitcast(FP8X4), zsc[:], z[:])
-            acc = ps.tile([P, PACK, HALF_V], F32, name="acc_out%d" % h)
-            for t in range(PACK):
-                nc.tensor.matmul_mx(acc[:, t, :], lhsT=w2w[:, 2 * P * t : 2 * P * (t + 1)].bitcast(FP4X4),
-                                    lhsT_scale=w2s[:, P * t : P * (t + 1)],
-                                    rhs=zw[:].bitcast(FP8X4), rhs_scale=zsc[:], start=True, stop=True)
             o = tile("o%d" % h, [P, PACK, HALF_V], F32)
-            nc.scalar.copy(o[:], acc[:])
+            per_bank = PACK if h == 0 else 2
+            for t0 in range(0, PACK, per_bank):
+                acc = ps.tile([P, per_bank, HALF_V], F32, name="acc_out%d_%d" % (h, t0))
+                for t in range(t0, t0 + per_bank):
+                    nc.tensor.matmul_mx(acc[:, t - t0, :], lhsT=w2w[:, 2 * P * t : 2 * P * (t + 1)].bitcast(FP4X4),
+                                        lhsT_scale=w2s[:, P * t : P * (t + 1)],
+                                        rhs=zw[:].bitcast(FP8X4), rhs_scale=zsc[:], start=True, stop=True)
+                nc.scalar.copy(o[:, t0 : t0 + per_bank, :], acc[:])
             nc.sync.dma_start(out_rows[:, :, vs], o[:])
             ob = tile("ob%d" % h, [P, PACK * HALF_V], BF16)
             nc.vector.tensor_copy(weave_dst(ob[:]), weave_src(o[:]))

@@ -45,7 +45,7 @@ def tile_picked_tropic_relu_po_kernel(
         p_t = [tile("p_t%d" % l, [P, V // 16], U16) for l in range(3)]
         xs_raw = reuse.tile([P, T], U8, name="xs_raw", offset=4032, align_bytes=64)
         xw_raw = tile("xw_raw", [P, T], U32)
-        w1_raw = reuse.tile([P, PACK, H], F32, name="w1_raw", offset=9728, align_bytes=64)
+        w1_raw = reuse.tile([P, PACK, H], F32, name="w1_raw", offset=7680, align_bytes=64)
 
         nc.vector.memset(xs_raw[:].bitcast(I32), 0)
 
@@ -61,11 +61,12 @@ def tile_picked_tropic_relu_po_kernel(
         xs = tile("xs", [P, S], U8)
         nc.vector.tensor_copy(xs[:], xs_raw[:].indirect(offs_t[:]))
 
-        src = w1_raw[:].rearrange("p j (m u e) -> p u m j e", u=2, e=2)
+        src = w1_raw[:].rearrange("p j (m u e) -> p u m e j", u=2, e=2)
         w1w = tile("w1w", [P, H], U32)
         w1s = tile("w1s", [P, H], U8)
-        w1_bf = [tile("w1_bf%d" % u, [P, 2 * H], BF16) for u in range(2)]
-        dst = [w[:].rearrange("p (e m j) -> p m j e", e=2, j=PACK) for w in w1_bf]
+        w1_bf = [tile("w1_bf0", [P, 2 * H], BF16),
+                 reuse.tile([P, 2 * H], BF16, name="w1_bf1", offset=5632, align_bytes=64)]
+        dst = [w[:].rearrange("p (e m j) -> p m e j", e=2, j=PACK) for w in w1_bf]
         nc.scalar.copy(dst[0], src[:, 0])
         nc.vector.tensor_copy(dst[1], src[:, 1])
         for u in (1, 0):
@@ -75,7 +76,7 @@ def tile_picked_tropic_relu_po_kernel(
         w2w_raw = reuse.tile([P, 2 * N], U8, name="w2w_raw", offset=4096, align_bytes=64)
         w2s_raw = reuse.tile([P, N], U8, name="w2s_raw", offset=5120, align_bytes=64)
         steps = [reuse.tile([P, PACK, V], F32, name="step%d" % l, offset=off, align_bytes=64)
-                 for l, off in enumerate((0, 5632, 9728))]
+                 for l, off in enumerate((0, 7680, 11776))]
         nc.vector.memset(w2s_raw[:].bitcast(I32), 0)
         nc.sync.dma_start(w2w_raw[:].bitcast(I32), w2_words[0].bitcast(I32))
         for l, tt in enumerate((t1, t2, t3)):
@@ -101,10 +102,10 @@ def tile_picked_tropic_relu_po_kernel(
 
         w2w = tile("w2w", [P, 2 * N], U8)
         w2s = tile("w2s", [P, N], U8)
-        nc.vector.tensor_copy(w2w[:].rearrange("p (t m b) -> p m t b", t=PACK, b=2),
-                              w2w_raw[:].rearrange("p (m t b) -> p m t b", t=PACK, b=2))
-        nc.vector.tensor_copy(w2s[:].rearrange("p (t m) -> p m t", t=PACK),
-                              w2s_raw[:].rearrange("p (m t) -> p m t", t=PACK))
+        nc.vector.tensor_copy(w2w[:].rearrange("p (t m b) -> p t m b", t=PACK, b=2),
+                              w2w_raw[:].rearrange("p (m t b) -> p t m b", t=PACK, b=2))
+        nc.vector.tensor_copy(w2s[:].rearrange("p (t m) -> p t m", t=PACK),
+                              w2s_raw[:].rearrange("p (m t) -> p t m", t=PACK))
 
         cand = []
         for l in range(2):
@@ -115,7 +116,9 @@ def tile_picked_tropic_relu_po_kernel(
             nc.scalar.activation(weave_dst(b[:]), weave_src(a[:]), ACT.Relu)
             cand.append(b)
         best2 = tile("best2", [P, PACK * V], BF16)
-        nc.vector.tensor_tensor(best2[:], cand[0][:], cand[1][:], ALU.max)
+        for h in range(2):
+            zs = slice(h * PACK * HALF_V, (h + 1) * PACK * HALF_V)
+            nc.vector.tensor_tensor(best2[:, zs], cand[0][:, zs], cand[1][:, zs], ALU.max)
 
         ow = tile("ow", [P, V], U32)
         osc = tile("osc", [P, V], U8)
@@ -128,12 +131,9 @@ def tile_picked_tropic_relu_po_kernel(
             for t in range(PACK):
                 nc.vector.tensor_tensor(a[:, t, :], y[t][:].indirect(p_t[2][:, h * 8 : (h + 1) * 8]), steps[2][:, t, vs], ALU.add)
             z = tile("z%d" % h, [P, PACK * HALF_V], BF16)
-            if h == 0:
-                b = tile("b2", [P, PACK * HALF_V], BF16)
-                nc.scalar.copy(weave_dst(b[:]), weave_src(a[:]))
-                nc.vector.tensor_tensor(z[:], b[:], best2[:, zs], ALU.max)
-            else:
-                nc.vector.tensor_tensor(weave_dst(z[:]), weave_src(a[:]), weave_dst(best2[:, zs]), ALU.max)
+            b = tile("b2_%d" % h, [P, PACK * HALF_V], BF16)
+            nc.scalar.copy(weave_dst(b[:]), weave_src(a[:]))
+            nc.vector.tensor_tensor(z[:], b[:], best2[:, zs], ALU.max)
             zw = tile("zw%d" % h, [P, HALF_V], U32)
             zsc = tile("zsc%d" % h, [P, HALF_V], U8)
             nc.vector.quantize_mx(zw[:].bitcast(FP8X4), zsc[:], z[:])

@@ -14,19 +14,39 @@ ALU = mybir.AluOpType
 ACT = mybir.ActivationFunctionType
 
 P = 128
-PACK = 4
+SLOTS = 4
+QUADRANTS = 4
+PER_COLUMN = 16
 K, T, S, V, N, H = 512, 2048, 512, 256, 512, 512
 HALF_S = S // 2
 HALF_V = V // 2
 FLOPS = 2 * K * H * S + 2 * H * N * V
 
+SCALAR_GROUPS = 80
 
-def weave_src(ap):
-    return ap.rearrange("p t (c i) -> p c t i", i=4)
+WORD_WINDOW = 0
+W1_ROUNDED = WORD_WINDOW + 4 * T
+SCALE_WINDOW = W1_ROUNDED + 2 * SLOTS * H
 
 
-def weave_dst(ap):
-    return ap.rearrange("p (c i t) -> p c t i", i=4, t=PACK)
+def slots_apart(ap):
+    return ap.rearrange("p t (c e) -> p c t e", e=4)
+
+
+def slots_together(ap):
+    return ap.rearrange("p (c e t) -> p c t e", e=4, t=SLOTS)
+
+
+def woven(columns):
+    return slice(SLOTS * columns.start, SLOTS * columns.stop)
+
+
+def scale_rows(tile, q):
+    return tile[32 * q : 32 * q + 4, :].bitcast(I32)
+
+
+def scale_rows_hbm(scales, q):
+    return scales[0, 4 * q : 4 * q + 4, :].bitcast(I32)
 
 
 def tile_picked_tropic_relu_po_kernel(
@@ -34,123 +54,157 @@ def tile_picked_tropic_relu_po_kernel(
 ):
     nc = tc.nc
     with ExitStack() as ctx:
-        sb = ctx.enter_context(tc.tile_pool(name="sb", bufs=1))
-        reuse = ctx.enter_context(tc.tile_pool(name="reuse", bufs=1))
-        ps = ctx.enter_context(tc.psum_pool(name="ps", bufs=1))
+        held = ctx.enter_context(tc.tile_pool(name="held", bufs=1))
+        shared = ctx.enter_context(tc.tile_pool(name="shared", bufs=1))
+        psum = ctx.enter_context(tc.psum_pool(name="psum", bufs=1))
 
-        def tile(name, shape, dtype):
-            return sb.tile(shape, dtype, name=name, align_bytes=64)
+        def own_tile(name, shape, dtype):
+            return held.tile(shape, dtype, name=name, align_bytes=64)
 
-        offs_t = tile("offs_t", [P, S // 16], U16)
-        p_t = [tile("p_t%d" % l, [P, V // 16], U16) for l in range(3)]
-        xs_raw = reuse.tile([P, T], U8, name="xs_raw", offset=4032, align_bytes=64)
-        xw_raw = tile("xw_raw", [P, T], U32)
-        w1_raw = reuse.tile([P, PACK, H], F32, name="w1_raw", offset=7680, align_bytes=64)
+        def shared_tile(name, shape, dtype, offset):
+            return shared.tile(shape, dtype, name=name, offset=offset, align_bytes=64)
 
-        nc.vector.memset(xs_raw[:].bitcast(I32), 0)
+        picks = own_tile("picks", [P, S // PER_COLUMN], U16)
+        lists = [own_tile("list%d" % l, [P, V // PER_COLUMN], U16) for l in range(3)]
+        x_scales_all = shared_tile("x_scales_all", [P, T], U8, SCALE_WINDOW)
+        x_words_all = shared_tile("x_words_all", [P, T], U32, WORD_WINDOW)
+        w1_raw = own_tile("w1_raw", [P, SLOTS, H], F32)
+        w2_words_raw = own_tile("w2_words_raw", [P, 2 * N], U8)
+        w2_scales_raw = own_tile("w2_scales_raw", [P, N], U8)
+        steps = [own_tile("step%d" % l, [P, SLOTS, V], F32) for l in range(3)]
 
-        nc.sync.dma_start(offs_t[:], offs)
-        nc.sync.dma_start(p_t[0][:], p1)
-        nc.sync.dma_start(w1_raw[:], w1.rearrange("(p j) c -> p j c", j=PACK))
-        nc.sync.dma_start(p_t[1][:], p2)
-        nc.sync.dma_start(xw_raw[:].bitcast(I32), x_words[0].rearrange("p n t -> p (n t)").bitcast(I32))
-        nc.sync.dma_start(p_t[2][:], p3)
-        for q in range(4):
-            nc.scalar.dma_start(xs_raw[32 * q : 32 * q + 4, :].bitcast(I32), x_scales[0, 4 * q : 4 * q + 4, :].bitcast(I32))
+        nc.vector.memset(x_scales_all[:].bitcast(I32), 0)
+        nc.vector.memset(w2_scales_raw[:].bitcast(I32), 0)
 
-        xs = tile("xs", [P, S], U8)
-        nc.vector.tensor_copy(xs[:], xs_raw[:].indirect(offs_t[:]))
+        step_rows = [t.rearrange("(p t) v -> p t v", t=SLOTS) for t in (t1, t2, t3)]
+        nc.sync.dma_start(w1_raw[:], w1.rearrange("(p j) c -> p j c", j=SLOTS))
+        nc.sync.dma_start(picks[:], offs)
+        nc.sync.dma_start(lists[0][:], p1)
+        for q in range(QUADRANTS):
+            nc.sync.dma_start(scale_rows(x_scales_all, q), scale_rows_hbm(x_scales, q))
+        nc.sync.dma_start(x_words_all[:].bitcast(I32), x_words[0].rearrange("p n t -> p (n t)").bitcast(I32))
+        nc.sync.dma_start(lists[1][:], p2)
+        nc.sync.dma_start(w2_words_raw[:].bitcast(I32), w2_words[0].bitcast(I32))
+        for q in range(QUADRANTS):
+            nc.sync.dma_start(scale_rows(w2_scales_raw, q), scale_rows_hbm(w2_scales, q))
+        nc.sync.dma_start(steps[0][:], step_rows[0])
+        nc.sync.dma_start(lists[2][:], p3)
+        nc.sync.dma_start(steps[1][:], step_rows[1])
+        nc.sync.dma_start(steps[2][:], step_rows[2])
 
-        src = w1_raw[:].rearrange("p j (m u e) -> p u m e j", u=2, e=2)
-        w1w = tile("w1w", [P, H], U32)
-        w1s = tile("w1s", [P, H], U8)
-        w1_bf = [tile("w1_bf0", [P, 2 * H], BF16),
-                 reuse.tile([P, 2 * H], BF16, name="w1_bf1", offset=5632, align_bytes=64)]
-        dst = [w[:].rearrange("p (e m j) -> p m e j", e=2, j=PACK) for w in w1_bf]
-        nc.scalar.copy(dst[0], src[:, 0])
-        nc.vector.tensor_copy(dst[1], src[:, 1])
-        for u in (1, 0):
-            cols = slice(2 * P * u, 2 * P * (u + 1))
-            nc.vector.quantize_mx(w1w[:, cols].bitcast(FP8X4), w1s[:, cols], w1_bf[u][:])
+        w1_from = w1_raw[:].rearrange("p j (m t) -> p m j t", t=SLOTS)
+        w1_words = shared_tile("w1_words", [P, H], U32, SCALE_WINDOW)
+        w1_scales = own_tile("w1_scales", [P, H], U8)
+        w1_rounded = shared_tile("w1_rounded", [P, SLOTS * H], BF16, W1_ROUNDED)
+        w1_to = w1_rounded[:].rearrange("p (t m j) -> p m j t", t=SLOTS, j=SLOTS)
+        nc.scalar.copy(w1_to[:, :SCALAR_GROUPS], w1_from[:, :SCALAR_GROUPS])
+        nc.vector.tensor_copy(w1_to[:, SCALAR_GROUPS:], w1_from[:, SCALAR_GROUPS:])
 
-        w2w_raw = reuse.tile([P, 2 * N], U8, name="w2w_raw", offset=4096, align_bytes=64)
-        w2s_raw = reuse.tile([P, N], U8, name="w2s_raw", offset=5120, align_bytes=64)
-        steps = [reuse.tile([P, PACK, V], F32, name="step%d" % l, offset=off, align_bytes=64)
-                 for l, off in enumerate((0, 7680, 11776))]
-        nc.vector.memset(w2s_raw[:].bitcast(I32), 0)
-        nc.sync.dma_start(w2w_raw[:].bitcast(I32), w2_words[0].bitcast(I32))
-        for l, tt in enumerate((t1, t2, t3)):
-            nc.sync.dma_start(steps[l][:], tt.rearrange("(p t) v -> p t v", t=PACK))
-        for q in range(4):
-            nc.sync.dma_start(w2s_raw[32 * q : 32 * q + 4, :].bitcast(I32), w2_scales[0, 4 * q : 4 * q + 4, :].bitcast(I32))
+        x_scales_picked = own_tile("x_scales_picked", [P, S], U8)
+        nc.vector.tensor_copy(x_scales_picked[:], x_scales_all[:].indirect(picks[:]))
 
-        xw = tile("xw", [P, S], U32)
-        y = [tile("y%d" % t, [P, S], F32) for t in range(PACK)]
+        nc.vector.quantize_mx(w1_words[:].bitcast(FP8X4), w1_scales[:], w1_rounded[:])
+
+        x_words_picked = shared_tile("x_words_picked", [P, S], U32, W1_ROUNDED)
+        y = [own_tile("y%d" % t, [P, S], F32) for t in range(SLOTS)]
+
+        def first_product(t, tokens, name):
+            features = slice(t * P, (t + 1) * P)
+            bank = psum.tile([P, tokens.stop - tokens.start], F32, name=name)
+            nc.tensor.matmul_mx(
+                bank[:],
+                lhsT=w1_words[:, features].bitcast(FP8X4),
+                lhsT_scale=w1_scales[:, features],
+                rhs=x_words_picked[:, tokens].bitcast(FP8X4),
+                rhs_scale=x_scales_picked[:, tokens],
+                start=True,
+                stop=True,
+            )
+            nc.scalar.copy(y[t][:, tokens], bank[:])
+
         for h in range(2):
-            cols = slice(h * HALF_S, (h + 1) * HALF_S)
-            nc.vector.tensor_copy(xw[:, cols], xw_raw[:].indirect(offs_t[:, h * 16 : (h + 1) * 16]))
-            acc = ps.tile([P, HALF_S], F32, name="acc_first%d" % h)
-            nc.tensor.matmul_mx(acc[:], lhsT=w1w[:, :P].bitcast(FP8X4), lhsT_scale=w1s[:, :P],
-                                rhs=xw[:, cols].bitcast(FP8X4), rhs_scale=xs[:, cols], start=True, stop=True)
-            nc.scalar.copy(y[0][:, cols], acc[:])
-        for t in range(1, PACK):
-            m = slice(t * P, (t + 1) * P)
-            acc = ps.tile([P, S], F32, name="acc%d" % t)
-            nc.tensor.matmul_mx(acc[:], lhsT=w1w[:, m].bitcast(FP8X4), lhsT_scale=w1s[:, m],
-                                rhs=xw[:].bitcast(FP8X4), rhs_scale=xs[:], start=True, stop=True)
-            nc.scalar.copy(y[t][:], acc[:])
+            tokens = slice(h * HALF_S, (h + 1) * HALF_S)
+            entries = picks[:, tokens.start // PER_COLUMN : tokens.stop // PER_COLUMN]
+            nc.vector.tensor_copy(x_words_picked[:, tokens], x_words_all[:].indirect(entries))
+            first_product(0, tokens, "y_bank0_%d" % h)
+        for t in range(1, SLOTS):
+            first_product(t, slice(0, S), "y_bank%d" % t)
 
-        w2w = tile("w2w", [P, 2 * N], U8)
-        w2s = tile("w2s", [P, N], U8)
-        nc.vector.tensor_copy(w2w[:].rearrange("p (t m b) -> p t m b", t=PACK, b=2),
-                              w2w_raw[:].rearrange("p (m t b) -> p t m b", t=PACK, b=2))
-        nc.vector.tensor_copy(w2s[:].rearrange("p (t m) -> p t m", t=PACK),
-                              w2s_raw[:].rearrange("p (m t) -> p t m", t=PACK))
+        w2_words_dealt = shared_tile("w2_words_dealt", [P, 2 * N], U8, WORD_WINDOW)
+        w2_scales_dealt = shared_tile("w2_scales_dealt", [P, N], U8, WORD_WINDOW + 2 * N)
+        nc.vector.tensor_copy(
+            w2_words_dealt[:].rearrange("p (t m b) -> p t m b", t=SLOTS, b=2),
+            w2_words_raw[:].rearrange("p (m t b) -> p t m b", t=SLOTS, b=2),
+        )
+        nc.vector.tensor_copy(
+            w2_scales_dealt[:].rearrange("p (t m) -> p t m", t=SLOTS),
+            w2_scales_raw[:].rearrange("p (m t) -> p t m", t=SLOTS),
+        )
 
-        cand = []
+        rounded = []
         for l in range(2):
-            a = tile("a%d" % l, [P, PACK, V], F32)
-            for t in range(PACK):
-                nc.vector.tensor_tensor(a[:, t, :], y[t][:].indirect(p_t[l][:]), steps[l][:, t, :], ALU.add)
-            b = tile("b%d" % l, [P, PACK * V], BF16)
-            nc.scalar.activation(weave_dst(b[:]), weave_src(a[:]), ACT.Relu)
-            cand.append(b)
-        best2 = tile("best2", [P, PACK * V], BF16)
-        for h in range(2):
-            zs = slice(h * PACK * HALF_V, (h + 1) * PACK * HALF_V)
-            nc.vector.tensor_tensor(best2[:, zs], cand[0][:, zs], cand[1][:, zs], ALU.max)
+            sums = own_tile("sums%d" % l, [P, SLOTS, V], F32)
+            for t in range(SLOTS):
+                nc.vector.tensor_tensor(sums[:, t, :], y[t][:].indirect(lists[l][:]), steps[l][:, t, :], ALU.add)
+            sums_rounded = own_tile("sums_rounded%d" % l, [P, SLOTS * V], BF16)
+            nc.scalar.activation(slots_together(sums_rounded[:]), slots_apart(sums[:]), ACT.Relu)
+            rounded.append(sums_rounded)
+        halves = [woven(slice(h * HALF_V, (h + 1) * HALF_V)) for h in range(2)]
+        best_of_two = own_tile("best_of_two", [P, SLOTS * V], BF16)
+        for half in halves:
+            nc.vector.tensor_tensor(best_of_two[:, half], rounded[0][:, half], rounded[1][:, half], ALU.max)
 
-        ow = tile("ow", [P, V], U32)
-        osc = tile("osc", [P, V], U8)
-        out_rows = out_0.rearrange("(p t) v -> p t v", t=PACK)
-        out_words = out_1[0].rearrange("p v b -> p (v b)").bitcast(I32)
+        parts = [slice(0, HALF_V // 2), slice(HALF_V // 2, HALF_V)]
+        out_words = own_tile("out_words", [P, V], U32)
+        out_scales = own_tile("out_scales", [P, V], U8)
+        out_rows_hbm = out_0.rearrange("(p t) v -> p t v", t=SLOTS)
+        out_words_hbm = out_1[0].rearrange("p v b -> p (v b)").bitcast(I32)
         for h in range(2):
-            vs = slice(h * HALF_V, (h + 1) * HALF_V)
-            zs = slice(h * PACK * HALF_V, (h + 1) * PACK * HALF_V)
-            a = tile("a2_%d" % h, [P, PACK, HALF_V], F32)
-            for t in range(PACK):
-                nc.vector.tensor_tensor(a[:, t, :], y[t][:].indirect(p_t[2][:, h * 8 : (h + 1) * 8]), steps[2][:, t, vs], ALU.add)
-            z = tile("z%d" % h, [P, PACK * HALF_V], BF16)
-            b = tile("b2_%d" % h, [P, PACK * HALF_V], BF16)
-            nc.scalar.copy(weave_dst(b[:]), weave_src(a[:]))
-            nc.vector.tensor_tensor(z[:], b[:], best2[:, zs], ALU.max)
-            zw = tile("zw%d" % h, [P, HALF_V], U32)
-            zsc = tile("zsc%d" % h, [P, HALF_V], U8)
-            nc.vector.quantize_mx(zw[:].bitcast(FP8X4), zsc[:], z[:])
-            o = tile("o%d" % h, [P, PACK, HALF_V], F32)
-            per_bank = PACK if h == 0 else 2
-            for t0 in range(0, PACK, per_bank):
-                acc = ps.tile([P, per_bank, HALF_V], F32, name="acc_out%d_%d" % (h, t0))
-                for t in range(t0, t0 + per_bank):
-                    nc.tensor.matmul_mx(acc[:, t - t0, :], lhsT=w2w[:, 2 * P * t : 2 * P * (t + 1)].bitcast(FP4X4),
-                                        lhsT_scale=w2s[:, P * t : P * (t + 1)],
-                                        rhs=zw[:].bitcast(FP8X4), rhs_scale=zsc[:], start=True, stop=True)
-                nc.scalar.copy(o[:, t0 : t0 + per_bank, :], acc[:])
-            nc.sync.dma_start(out_rows[:, :, vs], o[:])
-            ob = tile("ob%d" % h, [P, PACK * HALF_V], BF16)
-            nc.vector.tensor_copy(weave_dst(ob[:]), weave_src(o[:]))
-            nc.vector.quantize_mx(ow[:, vs].bitcast(FP8X4), osc[:, vs], ob[:])
-            nc.sync.dma_start(out_words[:, vs], ow[:, vs].bitcast(I32))
-        for q in range(4):
-            eng = nc.sync if q < 2 else nc.scalar
-            eng.dma_start(out_2[0, 4 * q : 4 * q + 4, :].bitcast(I32), osc[32 * q : 32 * q + 4, :].bitcast(I32))
+            states = slice(h * HALF_V, (h + 1) * HALF_V)
+            entries = lists[2][:, states.start // PER_COLUMN : states.stop // PER_COLUMN]
+            sums = own_tile("sums2_%d" % h, [P, SLOTS, HALF_V], F32)
+            for t in range(SLOTS):
+                nc.vector.tensor_tensor(sums[:, t, :], y[t][:].indirect(entries), steps[2][:, t, states], ALU.add)
+            z = own_tile("z%d" % h, [P, SLOTS * HALF_V], BF16)
+            sums_rounded = own_tile("sums_rounded2_%d" % h, [P, SLOTS * HALF_V], BF16)
+            nc.scalar.copy(slots_together(sums_rounded[:]), slots_apart(sums[:]))
+            best_here = best_of_two[:, halves[h]]
+            for part in parts:
+                flat = woven(part)
+                nc.vector.tensor_tensor(z[:, flat], sums_rounded[:, flat], best_here[:, flat], ALU.max)
+            z_words = own_tile("z_words%d" % h, [P, HALF_V], U32)
+            z_scales = own_tile("z_scales%d" % h, [P, HALF_V], U8)
+            for part in parts:
+                nc.vector.quantize_mx(z_words[:, part].bitcast(FP8X4), z_scales[:, part], z[:, woven(part)])
+
+            result = own_tile("result%d" % h, [P, SLOTS, HALF_V], F32)
+            per_bank = SLOTS // (h + 1)
+            for first in range(0, SLOTS, per_bank):
+                bank = psum.tile([P, per_bank, HALF_V], F32, name="out_bank%d_%d" % (h, first))
+                for t in range(first, first + per_bank):
+                    nc.tensor.matmul_mx(
+                        bank[:, t - first, :],
+                        lhsT=w2_words_dealt[:, 2 * P * t : 2 * P * (t + 1)].bitcast(FP4X4),
+                        lhsT_scale=w2_scales_dealt[:, P * t : P * (t + 1)],
+                        rhs=z_words[:].bitcast(FP8X4),
+                        rhs_scale=z_scales[:],
+                        start=True,
+                        stop=True,
+                    )
+                nc.scalar.copy(result[:, first : first + per_bank, :], bank[:])
+            nc.sync.dma_start(out_rows_hbm[:, :, states], result[:])
+
+            result_rounded = own_tile("result_rounded%d" % h, [P, SLOTS * HALF_V], BF16)
+            for part in parts:
+                nc.vector.tensor_copy(slots_together(result_rounded[:, woven(part)]), slots_apart(result[:, :, part]))
+            for part in parts:
+                nc.vector.quantize_mx(
+                    out_words[:, states][:, part].bitcast(FP8X4),
+                    out_scales[:, states][:, part],
+                    result_rounded[:, woven(part)],
+                )
+            nc.sync.dma_start(out_words_hbm[:, states], out_words[:, states].bitcast(I32))
+
+        for q in range(QUADRANTS):
+            queue = nc.sync if q < QUADRANTS // 2 else nc.scalar
+            queue.dma_start(scale_rows_hbm(out_2, q), scale_rows(out_scales, q))

@@ -18,15 +18,21 @@ SLOTS = 4
 QUADRANTS = 4
 PER_COLUMN = 16
 K, T, S, V, N, H = 512, 2048, 512, 256, 512, 512
+ROWS_AT = P - 16
 HALF_S = S // 2
 HALF_V = V // 2
 FLOPS = 2 * K * H * S + 2 * H * N * V
 
-SCALAR_GROUPS = 80
+SCALAR_GROUPS = 44
 
 WORD_WINDOW = 0
 W1_ROUNDED = WORD_WINDOW + 4 * T
-SCALE_WINDOW = W1_ROUNDED + 2 * SLOTS * H
+STEP_BYTES = 4 * SLOTS * V
+STEP1 = W1_ROUNDED + 2 * SLOTS * H
+SCALE_WINDOW = STEP1 + STEP_BYTES - 64
+W2_WORDS = SCALE_WINDOW + 64
+STEP2 = SCALE_WINDOW + T - 64
+W1_RAW = STEP2 + STEP_BYTES
 
 
 def slots_apart(ap):
@@ -41,12 +47,12 @@ def woven(columns):
     return slice(SLOTS * columns.start, SLOTS * columns.stop)
 
 
-def scale_rows(tile, q):
-    return tile[32 * q : 32 * q + 4, :].bitcast(I32)
+def scale_rows(tile, r):
+    return tile[r:P:32, :].bitcast(I32)
 
 
-def scale_rows_hbm(scales, q):
-    return scales[0, 4 * q : 4 * q + 4, :].bitcast(I32)
+def scale_rows_hbm(scales, r):
+    return scales[0, r:16:4, :].bitcast(I32)
 
 
 def tile_picked_tropic_relu_po_kernel(
@@ -68,40 +74,45 @@ def tile_picked_tropic_relu_po_kernel(
         lists = [own_tile("list%d" % l, [P, V // PER_COLUMN], U16) for l in range(3)]
         x_scales_all = shared_tile("x_scales_all", [P, T], U8, SCALE_WINDOW)
         x_words_all = shared_tile("x_words_all", [P, T], U32, WORD_WINDOW)
-        w1_raw = own_tile("w1_raw", [P, SLOTS, H], F32)
-        w2_words_raw = own_tile("w2_words_raw", [P, 2 * N], U8)
+        w1_raw = shared_tile("w1_raw", [P, SLOTS, H], F32, W1_RAW)
+        w2_words_raw = shared_tile("w2_words_raw", [P, 2 * N], U8, W2_WORDS)
         w2_scales_raw = own_tile("w2_scales_raw", [P, N], U8)
-        steps = [own_tile("step%d" % l, [P, SLOTS, V], F32) for l in range(3)]
+        steps = [
+            shared_tile("step%d" % l, [P, SLOTS, V], F32, offset) for l, offset in enumerate((STEP1, STEP2, W1_RAW))
+        ]
+        x_scales_picked = own_tile("x_scales_picked", [P, S], U8)
 
-        nc.vector.memset(x_scales_all[:].bitcast(I32), 0)
-        nc.vector.memset(w2_scales_raw[:].bitcast(I32), 0)
+        nc.vector.memset(x_scales_all[:ROWS_AT, :].bitcast(I32), 0)
+        nc.vector.memset(w2_scales_raw[:ROWS_AT, :].bitcast(I32), 0)
+        nc.vector.memset(x_scales_picked[:].bitcast(I32), 0)
+        w2_scales_placed = own_tile("w2_scales_placed", [P, N], U8)
+        nc.vector.memset(w2_scales_placed[:].bitcast(I32), 0)
 
         step_rows = [t.rearrange("(p t) v -> p t v", t=SLOTS) for t in (t1, t2, t3)]
-        nc.sync.dma_start(w1_raw[:], w1.rearrange("(p j) c -> p j c", j=SLOTS))
         nc.sync.dma_start(picks[:], offs)
-        nc.sync.dma_start(lists[0][:], p1)
-        for q in range(QUADRANTS):
-            nc.sync.dma_start(scale_rows(x_scales_all, q), scale_rows_hbm(x_scales, q))
+        nc.sync.dma_start(x_scales_all[ROWS_AT:, :].bitcast(I32), x_scales[0].bitcast(I32))
+        nc.sync.dma_start(w1_raw[:], w1.rearrange("(p j) c -> p j c", j=SLOTS))
+        for tile, source in zip(lists, (p1, p2, p3)):
+            nc.sync.dma_start(tile[:], source)
         nc.sync.dma_start(x_words_all[:].bitcast(I32), x_words[0].rearrange("p n t -> p (n t)").bitcast(I32))
-        nc.sync.dma_start(lists[1][:], p2)
+        nc.sync.dma_start(w2_scales_raw[ROWS_AT:, :].bitcast(I32), w2_scales[0].bitcast(I32))
+
+        x_scales_spread = own_tile("x_scales_spread", [P, S], U8)
+        nc.vector.tensor_copy(x_scales_spread[:], x_scales_all[:].indirect(picks[:]))
+        for r in range(QUADRANTS):
+            nc.sync.dma_start(scale_rows(x_scales_picked, r), x_scales_spread[ROWS_AT + r : P : 4, :].bitcast(I32))
         nc.sync.dma_start(w2_words_raw[:].bitcast(I32), w2_words[0].bitcast(I32))
-        for q in range(QUADRANTS):
-            nc.sync.dma_start(scale_rows(w2_scales_raw, q), scale_rows_hbm(w2_scales, q))
         nc.sync.dma_start(steps[0][:], step_rows[0])
-        nc.sync.dma_start(lists[2][:], p3)
         nc.sync.dma_start(steps[1][:], step_rows[1])
-        nc.sync.dma_start(steps[2][:], step_rows[2])
 
         w1_from = w1_raw[:].rearrange("p j (m t) -> p m j t", t=SLOTS)
-        w1_words = shared_tile("w1_words", [P, H], U32, SCALE_WINDOW)
+        w1_words = own_tile("w1_words", [P, H], U32)
         w1_scales = own_tile("w1_scales", [P, H], U8)
         w1_rounded = shared_tile("w1_rounded", [P, SLOTS * H], BF16, W1_ROUNDED)
         w1_to = w1_rounded[:].rearrange("p (t m j) -> p m j t", t=SLOTS, j=SLOTS)
         nc.scalar.copy(w1_to[:, :SCALAR_GROUPS], w1_from[:, :SCALAR_GROUPS])
         nc.vector.tensor_copy(w1_to[:, SCALAR_GROUPS:], w1_from[:, SCALAR_GROUPS:])
-
-        x_scales_picked = own_tile("x_scales_picked", [P, S], U8)
-        nc.vector.tensor_copy(x_scales_picked[:], x_scales_all[:].indirect(picks[:]))
+        nc.sync.dma_start(steps[2][:], step_rows[2])
 
         nc.vector.quantize_mx(w1_words[:].bitcast(FP8X4), w1_scales[:], w1_rounded[:])
 
@@ -140,6 +151,8 @@ def tile_picked_tropic_relu_po_kernel(
             w2_scales_dealt[:].rearrange("p (t m) -> p t m", t=SLOTS),
             w2_scales_raw[:].rearrange("p (m t) -> p t m", t=SLOTS),
         )
+        for r in range(QUADRANTS):
+            nc.sync.dma_start(scale_rows(w2_scales_placed, r), w2_scales_dealt[ROWS_AT + r : P : 4, :].bitcast(I32))
 
         rounded = []
         for l in range(2):
@@ -185,7 +198,7 @@ def tile_picked_tropic_relu_po_kernel(
                     nc.tensor.matmul_mx(
                         bank[:, t - first, :],
                         lhsT=w2_words_dealt[:, 2 * P * t : 2 * P * (t + 1)].bitcast(FP4X4),
-                        lhsT_scale=w2_scales_dealt[:, P * t : P * (t + 1)],
+                        lhsT_scale=w2_scales_placed[:, P * t : P * (t + 1)],
                         rhs=z_words[:].bitcast(FP8X4),
                         rhs_scale=z_scales[:],
                         start=True,

@@ -90,7 +90,7 @@ def tile_picked_tropic_relu_po_kernel(
 
         step_rows = [t.rearrange("(p t) v -> p t v", t=SLOTS) for t in (t1, t2, t3)]
         nc.sync.dma_start(picks[:], offs)
-        nc.sync.dma_start(x_scales_all[ROWS_AT:, :].bitcast(I32), x_scales[0].bitcast(I32))
+        nc.scalar.dma_start(x_scales_all[ROWS_AT:, :].bitcast(I32), x_scales[0].bitcast(I32))
         nc.sync.dma_start(w1_raw[:], w1.rearrange("(p j) c -> p j c", j=SLOTS))
         for tile, source in zip(lists, (p1, p2, p3)):
             nc.sync.dma_start(tile[:], source)
@@ -119,7 +119,7 @@ def tile_picked_tropic_relu_po_kernel(
         x_words_picked = shared_tile("x_words_picked", [P, S], U32, W1_ROUNDED)
         y = [own_tile("y%d" % t, [P, S], F32) for t in range(SLOTS)]
 
-        def first_product(t, tokens, name):
+        def first_product(t, tokens, name, copy_out):
             features = slice(t * P, (t + 1) * P)
             bank = psum.tile([P, tokens.stop - tokens.start], F32, name=name)
             nc.tensor.matmul_mx(
@@ -131,21 +131,24 @@ def tile_picked_tropic_relu_po_kernel(
                 start=True,
                 stop=True,
             )
-            nc.scalar.copy(y[t][:, tokens], bank[:])
+            copy_out(y[t][:, tokens], bank[:])
 
         for h in range(2):
             tokens = slice(h * HALF_S, (h + 1) * HALF_S)
             entries = picks[:, tokens.start // PER_COLUMN : tokens.stop // PER_COLUMN]
             nc.vector.tensor_copy(x_words_picked[:, tokens], x_words_all[:].indirect(entries))
-            first_product(0, tokens, "y_bank0_%d" % h)
+            if h == 0:
+                first_product(0, tokens, "bank0", nc.scalar.copy)
+        first_product(0, slice(HALF_S, HALF_S + P), "bank1", nc.vector.tensor_copy)
+        first_product(0, slice(HALF_S + P, S), "bank5", nc.scalar.copy)
         for t in range(1, SLOTS):
-            first_product(t, slice(0, S), "y_bank%d" % t)
+            first_product(t, slice(0, S), "bank%d" % (t + 1), nc.scalar.copy)
 
         w2_words_dealt = shared_tile("w2_words_dealt", [P, 2 * N], U8, WORD_WINDOW)
         w2_scales_dealt = shared_tile("w2_scales_dealt", [P, N], U8, WORD_WINDOW + 2 * N)
         nc.vector.tensor_copy(
-            w2_words_dealt[:].rearrange("p (t m b) -> p t m b", t=SLOTS, b=2),
-            w2_words_raw[:].rearrange("p (m t b) -> p t m b", t=SLOTS, b=2),
+            w2_words_dealt[:].bitcast(U16).rearrange("p (t m) -> p t m", t=SLOTS),
+            w2_words_raw[:].bitcast(U16).rearrange("p (m t) -> p t m", t=SLOTS),
         )
         nc.vector.tensor_copy(
             w2_scales_dealt[:].rearrange("p (t m) -> p t m", t=SLOTS),
@@ -154,14 +157,13 @@ def tile_picked_tropic_relu_po_kernel(
         for r in range(QUADRANTS):
             nc.sync.dma_start(scale_rows(w2_scales_placed, r), w2_scales_dealt[ROWS_AT + r : P : 4, :].bitcast(I32))
 
-        rounded = []
+        sums12 = [own_tile("sums%d" % l, [P, SLOTS, V], F32) for l in range(2)]
+        order = [(0, 0), (1, 0)] + [(l, t) for l in range(2) for t in range(1, SLOTS)]
+        for l, t in order:
+            nc.vector.tensor_tensor(sums12[l][:, t, :], y[t][:].indirect(lists[l][:]), steps[l][:, t, :], ALU.add)
+        rounded = [own_tile("sums_rounded%d" % l, [P, SLOTS * V], BF16) for l in range(2)]
         for l in range(2):
-            sums = own_tile("sums%d" % l, [P, SLOTS, V], F32)
-            for t in range(SLOTS):
-                nc.vector.tensor_tensor(sums[:, t, :], y[t][:].indirect(lists[l][:]), steps[l][:, t, :], ALU.add)
-            sums_rounded = own_tile("sums_rounded%d" % l, [P, SLOTS * V], BF16)
-            nc.scalar.activation(slots_together(sums_rounded[:]), slots_apart(sums[:]), ACT.Relu)
-            rounded.append(sums_rounded)
+            nc.scalar.activation(slots_together(rounded[l][:]), slots_apart(sums12[l][:]), ACT.Relu)
         halves = [woven(slice(h * HALF_V, (h + 1) * HALF_V)) for h in range(2)]
         best_of_two = own_tile("best_of_two", [P, SLOTS * V], BF16)
         for half in halves:
@@ -180,7 +182,8 @@ def tile_picked_tropic_relu_po_kernel(
                 nc.vector.tensor_tensor(sums[:, t, :], y[t][:].indirect(entries), steps[2][:, t, states], ALU.add)
             z = own_tile("z%d" % h, [P, SLOTS * HALF_V], BF16)
             sums_rounded = own_tile("sums_rounded2_%d" % h, [P, SLOTS * HALF_V], BF16)
-            nc.scalar.copy(slots_together(sums_rounded[:]), slots_apart(sums[:]))
+            for part in parts if h == 1 else [slice(0, HALF_V)]:
+                nc.scalar.copy(slots_together(sums_rounded[:, woven(part)]), slots_apart(sums[:, :, part]))
             best_here = best_of_two[:, halves[h]]
             for part in parts:
                 flat = woven(part)
@@ -191,9 +194,9 @@ def tile_picked_tropic_relu_po_kernel(
                 nc.vector.quantize_mx(z_words[:, part].bitcast(FP8X4), z_scales[:, part], z[:, woven(part)])
 
             result = own_tile("result%d" % h, [P, SLOTS, HALF_V], F32)
-            per_bank = SLOTS // (h + 1)
+            per_bank = SLOTS // 2
             for first in range(0, SLOTS, per_bank):
-                bank = psum.tile([P, per_bank, HALF_V], F32, name="out_bank%d_%d" % (h, first))
+                bank = psum.tile([P, per_bank, HALF_V], F32, name="bank%d" % (2 * h + first // per_bank))
                 for t in range(first, first + per_bank):
                     nc.tensor.matmul_mx(
                         bank[:, t - first, :],

@@ -91,11 +91,12 @@ def tile_picked_tropic_relu_po_kernel(
         step_rows = [t.rearrange("(p t) v -> p t v", t=SLOTS) for t in (t1, t2, t3)]
         nc.sync.dma_start(picks[:], offs)
         nc.scalar.dma_start(x_scales_all[ROWS_AT:, :].bitcast(I32), x_scales[0].bitcast(I32))
+        nc.scalar.dma_start(w2_scales_raw[ROWS_AT:, :].bitcast(I32), w2_scales[0].bitcast(I32))
         nc.sync.dma_start(w1_raw[:], w1.rearrange("(p j) c -> p j c", j=SLOTS))
-        for tile, source in zip(lists, (p1, p2, p3)):
-            nc.sync.dma_start(tile[:], source)
+        nc.sync.dma_start(lists[0][:], p1)
+        nc.sync.dma_start(lists[1][:], p2)
         nc.sync.dma_start(x_words_all[:].bitcast(I32), x_words[0].rearrange("p n t -> p (n t)").bitcast(I32))
-        nc.sync.dma_start(w2_scales_raw[ROWS_AT:, :].bitcast(I32), w2_scales[0].bitcast(I32))
+        nc.sync.dma_start(lists[2][:], p3)
 
         x_scales_spread = own_tile("x_scales_spread", [P, S], U8)
         nc.vector.tensor_copy(x_scales_spread[:], x_scales_all[:].indirect(picks[:]))
@@ -211,8 +212,13 @@ def tile_picked_tropic_relu_po_kernel(
             nc.sync.dma_start(out_rows_hbm[:, :, states], result[:])
 
             result_rounded = own_tile("result_rounded%d" % h, [P, SLOTS * HALF_V], BF16)
-            for part in parts:
-                nc.vector.tensor_copy(slots_together(result_rounded[:, woven(part)]), slots_apart(result[:, :, part]))
+            pairs = [slice(0, SLOTS)] if h == 0 else [slice(0, 2), slice(2, 4)]
+            for pair in pairs:
+                for part in parts:
+                    nc.vector.tensor_copy(
+                        slots_together(result_rounded[:, woven(part)])[:, :, pair, :],
+                        slots_apart(result[:, pair, part]),
+                    )
             for part in parts:
                 nc.vector.quantize_mx(
                     out_words[:, states][:, part].bitcast(FP8X4),

@@ -15,23 +15,27 @@ ACT = mybir.ActivationFunctionType
 
 P = 128
 SLOTS = 4
-QUADRANTS = 4
+QUADRANT = 32
+ROWS = 4
 PER_COLUMN = 16
 K, T, S, V, N, H = 512, 2048, 512, 256, 512, 512
-ROWS_AT = P - 16
+ALL_ROWS = ROWS * P // QUADRANT
+ROWS_AT = P - ALL_ROWS
 HALF_S = S // 2
+QUARTER_S = S // 4
 HALF_V = V // 2
 FLOPS = 2 * K * H * S + 2 * H * N * V
 
 SCALAR_GROUPS = 44
 
+OVERLAP = 64
+STEP_BYTES = 4 * SLOTS * V
 WORD_WINDOW = 0
 W1_ROUNDED = WORD_WINDOW + 4 * T
-STEP_BYTES = 4 * SLOTS * V
 STEP1 = W1_ROUNDED + 2 * SLOTS * H
-SCALE_WINDOW = STEP1 + STEP_BYTES - 64
-W2_WORDS = SCALE_WINDOW + 64
-STEP2 = SCALE_WINDOW + T - 64
+SCALE_WINDOW = STEP1 + STEP_BYTES - OVERLAP
+W2_WORDS = SCALE_WINDOW + OVERLAP
+STEP2 = SCALE_WINDOW + T - OVERLAP
 W1_RAW = STEP2 + STEP_BYTES
 
 
@@ -47,12 +51,16 @@ def woven(columns):
     return slice(SLOTS * columns.start, SLOTS * columns.stop)
 
 
-def scale_rows(tile, r):
-    return tile[r:P:32, :].bitcast(I32)
+def placed_rows(tile, r):
+    return tile[r:P:QUADRANT, :].bitcast(I32)
 
 
-def scale_rows_hbm(scales, r):
-    return scales[0, r:16:4, :].bitcast(I32)
+def loaded_rows(tile, r):
+    return tile[ROWS_AT + r : P : ROWS, :].bitcast(I32)
+
+
+def hbm_rows(scales, r):
+    return scales[0, r:ALL_ROWS:ROWS, :].bitcast(I32)
 
 
 def tile_picked_tropic_relu_po_kernel(
@@ -85,8 +93,6 @@ def tile_picked_tropic_relu_po_kernel(
         nc.vector.memset(x_scales_all[:ROWS_AT, :].bitcast(I32), 0)
         nc.vector.memset(w2_scales_raw[:ROWS_AT, :].bitcast(I32), 0)
         nc.vector.memset(x_scales_picked[:].bitcast(I32), 0)
-        w2_scales_placed = own_tile("w2_scales_placed", [P, N], U8)
-        nc.vector.memset(w2_scales_placed[:].bitcast(I32), 0)
 
         step_rows = [t.rearrange("(p t) v -> p t v", t=SLOTS) for t in (t1, t2, t3)]
         nc.sync.dma_start(picks[:], offs)
@@ -98,10 +104,10 @@ def tile_picked_tropic_relu_po_kernel(
         nc.sync.dma_start(x_words_all[:].bitcast(I32), x_words[0].rearrange("p n t -> p (n t)").bitcast(I32))
         nc.sync.dma_start(lists[2][:], p3)
 
-        x_scales_spread = own_tile("x_scales_spread", [P, S], U8)
-        nc.vector.tensor_copy(x_scales_spread[:], x_scales_all[:].indirect(picks[:]))
-        for r in range(QUADRANTS):
-            nc.sync.dma_start(scale_rows(x_scales_picked, r), x_scales_spread[ROWS_AT + r : P : 4, :].bitcast(I32))
+        x_scales_gathered = own_tile("x_scales_gathered", [P, S], U8)
+        nc.vector.tensor_copy(x_scales_gathered[:], x_scales_all[:].indirect(picks[:]))
+        for r in range(ROWS):
+            nc.sync.dma_start(placed_rows(x_scales_picked, r), loaded_rows(x_scales_gathered, r))
         nc.sync.dma_start(w2_words_raw[:].bitcast(I32), w2_words[0].bitcast(I32))
         nc.sync.dma_start(steps[0][:], step_rows[0])
         nc.sync.dma_start(steps[1][:], step_rows[1])
@@ -120,9 +126,9 @@ def tile_picked_tropic_relu_po_kernel(
         x_words_picked = shared_tile("x_words_picked", [P, S], U32, W1_ROUNDED)
         y = [own_tile("y%d" % t, [P, S], F32) for t in range(SLOTS)]
 
-        def first_product(t, tokens, name, copy_out):
+        def first_product(t, tokens, bank_number, copy_out):
             features = slice(t * P, (t + 1) * P)
-            bank = psum.tile([P, tokens.stop - tokens.start], F32, name=name)
+            bank = psum.tile([P, tokens.stop - tokens.start], F32, name="bank%d" % bank_number)
             nc.tensor.matmul_mx(
                 bank[:],
                 lhsT=w1_words[:, features].bitcast(FP8X4),
@@ -134,19 +140,25 @@ def tile_picked_tropic_relu_po_kernel(
             )
             copy_out(y[t][:, tokens], bank[:])
 
-        for h in range(2):
-            tokens = slice(h * HALF_S, (h + 1) * HALF_S)
+        def gather_words(tokens):
             entries = picks[:, tokens.start // PER_COLUMN : tokens.stop // PER_COLUMN]
             nc.vector.tensor_copy(x_words_picked[:, tokens], x_words_all[:].indirect(entries))
-            if h == 0:
-                first_product(0, tokens, "bank0", nc.scalar.copy)
-        first_product(0, slice(HALF_S, HALF_S + P), "bank1", nc.vector.tensor_copy)
-        first_product(0, slice(HALF_S + P, S), "bank5", nc.scalar.copy)
-        for t in range(1, SLOTS):
-            first_product(t, slice(0, S), "bank%d" % (t + 1), nc.scalar.copy)
+
+        first_half, second_half = slice(0, HALF_S), slice(HALF_S, S)
+        gather_words(first_half)
+        first_product(0, first_half, 0, nc.scalar.copy)
+        first_product(1, first_half, 1, nc.scalar.copy)
+        gather_words(second_half)
+        first_product(0, slice(HALF_S, HALF_S + QUARTER_S), 2, nc.vector.tensor_copy)
+        first_product(0, slice(HALF_S + QUARTER_S, S), 3, nc.scalar.copy)
+        first_product(1, second_half, 4, nc.scalar.copy)
+        first_product(2, slice(0, S), 5, nc.scalar.copy)
+        first_product(3, slice(0, S), 6, nc.scalar.copy)
 
         w2_words_dealt = shared_tile("w2_words_dealt", [P, 2 * N], U8, WORD_WINDOW)
-        w2_scales_dealt = shared_tile("w2_scales_dealt", [P, N], U8, WORD_WINDOW + 2 * N)
+        w2_scales_dealt = own_tile("w2_scales_dealt", [P, N], U8)
+        w2_scales_placed = shared_tile("w2_scales_placed", [P, N], U8, WORD_WINDOW + 2 * N)
+        nc.vector.memset(w2_scales_placed[:].bitcast(I32), 0)
         nc.vector.tensor_copy(
             w2_words_dealt[:].bitcast(U16).rearrange("p (t m) -> p t m", t=SLOTS),
             w2_words_raw[:].bitcast(U16).rearrange("p (m t) -> p t m", t=SLOTS),
@@ -155,27 +167,32 @@ def tile_picked_tropic_relu_po_kernel(
             w2_scales_dealt[:].rearrange("p (t m) -> p t m", t=SLOTS),
             w2_scales_raw[:].rearrange("p (m t) -> p t m", t=SLOTS),
         )
-        for r in range(QUADRANTS):
-            nc.sync.dma_start(scale_rows(w2_scales_placed, r), w2_scales_dealt[ROWS_AT + r : P : 4, :].bitcast(I32))
+        for r in range(ROWS):
+            nc.sync.dma_start(placed_rows(w2_scales_placed, r), loaded_rows(w2_scales_dealt, r))
 
-        sums12 = [own_tile("sums%d" % l, [P, SLOTS, V], F32) for l in range(2)]
-        order = [(0, 0), (1, 0)] + [(l, t) for l in range(2) for t in range(1, SLOTS)]
-        for l, t in order:
-            nc.vector.tensor_tensor(sums12[l][:, t, :], y[t][:].indirect(lists[l][:]), steps[l][:, t, :], ALU.add)
+        step_sums = [own_tile("sums%d" % l, [P, SLOTS, V], F32) for l in range(2)]
+        for l in range(2):
+            for t in range(SLOTS):
+                looked_up = y[t][:].indirect(lists[l][:])
+                nc.vector.tensor_tensor(step_sums[l][:, t, :], looked_up, steps[l][:, t, :], ALU.add)
         rounded = [own_tile("sums_rounded%d" % l, [P, SLOTS * V], BF16) for l in range(2)]
         for l in range(2):
-            nc.scalar.activation(slots_together(rounded[l][:]), slots_apart(sums12[l][:]), ACT.Relu)
+            nc.scalar.activation(slots_together(rounded[l][:]), slots_apart(step_sums[l][:]), ACT.Relu)
         halves = [woven(slice(h * HALF_V, (h + 1) * HALF_V)) for h in range(2)]
         best_of_two = own_tile("best_of_two", [P, SLOTS * V], BF16)
         for half in halves:
             nc.vector.tensor_tensor(best_of_two[:, half], rounded[0][:, half], rounded[1][:, half], ALU.max)
 
         parts = [slice(0, HALF_V // 2), slice(HALF_V // 2, HALF_V)]
+        whole_half = [slice(0, HALF_V)]
+        pairs = [slice(0, SLOTS // 2), slice(SLOTS // 2, SLOTS)]
+        all_slots = [slice(0, SLOTS)]
         out_words = own_tile("out_words", [P, V], U32)
         out_scales = own_tile("out_scales", [P, V], U8)
         out_rows_hbm = out_0.rearrange("(p t) v -> p t v", t=SLOTS)
         out_words_hbm = out_1[0].rearrange("p v b -> p (v b)").bitcast(I32)
         for h in range(2):
+            last_half = h == 1
             states = slice(h * HALF_V, (h + 1) * HALF_V)
             entries = lists[2][:, states.start // PER_COLUMN : states.stop // PER_COLUMN]
             sums = own_tile("sums2_%d" % h, [P, SLOTS, HALF_V], F32)
@@ -183,7 +200,7 @@ def tile_picked_tropic_relu_po_kernel(
                 nc.vector.tensor_tensor(sums[:, t, :], y[t][:].indirect(entries), steps[2][:, t, states], ALU.add)
             z = own_tile("z%d" % h, [P, SLOTS * HALF_V], BF16)
             sums_rounded = own_tile("sums_rounded2_%d" % h, [P, SLOTS * HALF_V], BF16)
-            for part in parts if h == 1 else [slice(0, HALF_V)]:
+            for part in parts if last_half else whole_half:
                 nc.scalar.copy(slots_together(sums_rounded[:, woven(part)]), slots_apart(sums[:, :, part]))
             best_here = best_of_two[:, halves[h]]
             for part in parts:
@@ -195,12 +212,11 @@ def tile_picked_tropic_relu_po_kernel(
                 nc.vector.quantize_mx(z_words[:, part].bitcast(FP8X4), z_scales[:, part], z[:, woven(part)])
 
             result = own_tile("result%d" % h, [P, SLOTS, HALF_V], F32)
-            per_bank = SLOTS // 2
-            for first in range(0, SLOTS, per_bank):
-                bank = psum.tile([P, per_bank, HALF_V], F32, name="bank%d" % (2 * h + first // per_bank))
-                for t in range(first, first + per_bank):
+            for g, pair in enumerate(pairs):
+                bank = psum.tile([P, SLOTS // 2, HALF_V], F32, name="bank%d" % (len(pairs) * h + g))
+                for t in range(pair.start, pair.stop):
                     nc.tensor.matmul_mx(
-                        bank[:, t - first, :],
+                        bank[:, t - pair.start, :],
                         lhsT=w2_words_dealt[:, 2 * P * t : 2 * P * (t + 1)].bitcast(FP4X4),
                         lhsT_scale=w2_scales_placed[:, P * t : P * (t + 1)],
                         rhs=z_words[:].bitcast(FP8X4),
@@ -208,16 +224,15 @@ def tile_picked_tropic_relu_po_kernel(
                         start=True,
                         stop=True,
                     )
-                nc.scalar.copy(result[:, first : first + per_bank, :], bank[:])
+                nc.scalar.copy(result[:, pair, :], bank[:])
             nc.sync.dma_start(out_rows_hbm[:, :, states], result[:])
 
             result_rounded = own_tile("result_rounded%d" % h, [P, SLOTS * HALF_V], BF16)
-            pairs = [slice(0, SLOTS)] if h == 0 else [slice(0, 2), slice(2, 4)]
-            for pair in pairs:
+            for slots in pairs if last_half else all_slots:
                 for part in parts:
                     nc.vector.tensor_copy(
-                        slots_together(result_rounded[:, woven(part)])[:, :, pair, :],
-                        slots_apart(result[:, pair, part]),
+                        slots_together(result_rounded[:, woven(part)])[:, :, slots, :],
+                        slots_apart(result[:, slots, part]),
                     )
             for part in parts:
                 nc.vector.quantize_mx(
@@ -227,6 +242,6 @@ def tile_picked_tropic_relu_po_kernel(
                 )
             nc.sync.dma_start(out_words_hbm[:, states], out_words[:, states].bitcast(I32))
 
-        for q in range(QUADRANTS):
-            queue = nc.sync if q < QUADRANTS // 2 else nc.scalar
-            queue.dma_start(scale_rows_hbm(out_2, q), scale_rows(out_scales, q))
+        for r in range(ROWS):
+            queue = nc.sync if r < ROWS // 2 else nc.scalar
+            queue.dma_start(hbm_rows(out_2, r), placed_rows(out_scales, r))

@@ -170,21 +170,32 @@ def tile_picked_tropic_relu_po_kernel(
         for r in range(ROWS):
             nc.sync.dma_start(placed_rows(w2_scales_placed, r), loaded_rows(w2_scales_dealt, r))
 
+        third = own_tile("third", [P, SLOTS, V], F32)
         step_sums = [own_tile("sums%d" % l, [P, SLOTS, V], F32) for l in range(2)]
+        for t in range(SLOTS):
+            nc.scalar.activation(third[:, t, :], y[t][:].indirect(lists[2][:]), ACT.Copy)
         for l in range(2):
             for t in range(SLOTS):
                 looked_up = y[t][:].indirect(lists[l][:])
                 nc.vector.tensor_tensor(step_sums[l][:, t, :], looked_up, steps[l][:, t, :], ALU.add)
-        rounded = [own_tile("sums_rounded%d" % l, [P, SLOTS * V], BF16) for l in range(2)]
-        for l in range(2):
-            nc.scalar.activation(slots_together(rounded[l][:]), slots_apart(step_sums[l][:]), ACT.Relu)
-        halves = [woven(slice(h * HALF_V, (h + 1) * HALF_V)) for h in range(2)]
+        columns = [slice(h * HALF_V, (h + 1) * HALF_V) for h in range(2)]
+        halves = [woven(c) for c in columns]
+        rounded = [own_tile("sums_rounded%d" % l, [P, SLOTS * V], BF16) for l in range(3)]
+        nc.scalar.activation(slots_together(rounded[0][:]), slots_apart(step_sums[0][:]), ACT.Relu)
+        for h in range(2):
+            nc.scalar.copy(slots_together(rounded[1][:, halves[h]]), slots_apart(step_sums[1][:, :, columns[h]]))
+        for h in range(2):
+            nc.vector.tensor_tensor(
+                slots_together(rounded[2][:, halves[h]]),
+                slots_apart(third[:, :, columns[h]]),
+                slots_apart(steps[2][:, :, columns[h]]),
+                ALU.add,
+            )
         best_of_two = own_tile("best_of_two", [P, SLOTS * V], BF16)
         for half in halves:
-            nc.vector.tensor_tensor(best_of_two[:, half], rounded[0][:, half], rounded[1][:, half], ALU.max)
+            nc.vector.tensor_tensor(best_of_two[:, half], rounded[0][:, half], rounded[2][:, half], ALU.max)
 
         parts = [slice(0, HALF_V // 2), slice(HALF_V // 2, HALF_V)]
-        whole_half = [slice(0, HALF_V)]
         pairs = [slice(0, SLOTS // 2), slice(SLOTS // 2, SLOTS)]
         all_slots = [slice(0, SLOTS)]
         out_words = own_tile("out_words", [P, V], U32)
@@ -193,19 +204,13 @@ def tile_picked_tropic_relu_po_kernel(
         out_words_hbm = out_1[0].rearrange("p v b -> p (v b)").bitcast(I32)
         for h in range(2):
             last_half = h == 1
-            states = slice(h * HALF_V, (h + 1) * HALF_V)
-            entries = lists[2][:, states.start // PER_COLUMN : states.stop // PER_COLUMN]
-            sums = own_tile("sums2_%d" % h, [P, SLOTS, HALF_V], F32)
-            for t in range(SLOTS):
-                nc.vector.tensor_tensor(sums[:, t, :], y[t][:].indirect(entries), steps[2][:, t, states], ALU.add)
+            states = columns[h]
             z = own_tile("z%d" % h, [P, SLOTS * HALF_V], BF16)
-            sums_rounded = own_tile("sums_rounded2_%d" % h, [P, SLOTS * HALF_V], BF16)
-            for part in parts if last_half else whole_half:
-                nc.scalar.copy(slots_together(sums_rounded[:, woven(part)]), slots_apart(sums[:, :, part]))
+            second_here = rounded[1][:, halves[h]]
             best_here = best_of_two[:, halves[h]]
             for part in parts:
                 flat = woven(part)
-                nc.vector.tensor_tensor(z[:, flat], sums_rounded[:, flat], best_here[:, flat], ALU.max)
+                nc.vector.tensor_tensor(z[:, flat], second_here[:, flat], best_here[:, flat], ALU.max)
             z_words = own_tile("z_words%d" % h, [P, HALF_V], U32)
             z_scales = own_tile("z_scales%d" % h, [P, HALF_V], U8)
             for part in parts:

@@ -180,42 +180,52 @@ def tile_picked_tropic_relu_po_kernel(
                 nc.vector.tensor_tensor(step_sums[l][:, t, :], looked_up, steps[l][:, t, :], ALU.add)
         columns = [slice(h * HALF_V, (h + 1) * HALF_V) for h in range(2)]
         halves = [woven(c) for c in columns]
-        rounded = [own_tile("sums_rounded%d" % l, [P, SLOTS * V], BF16) for l in range(3)]
+        rounded = [own_tile("sums_rounded%d" % l, [P, SLOTS * V], BF16) for l in range(2)]
         nc.scalar.activation(slots_together(rounded[0][:]), slots_apart(step_sums[0][:]), ACT.Relu)
         for h in range(2):
             nc.scalar.copy(slots_together(rounded[1][:, halves[h]]), slots_apart(step_sums[1][:, :, columns[h]]))
-        for h in range(2):
-            nc.vector.tensor_tensor(
-                slots_together(rounded[2][:, halves[h]]),
-                slots_apart(third[:, :, columns[h]]),
-                slots_apart(steps[2][:, :, columns[h]]),
-                ALU.add,
-            )
-        best_of_two = own_tile("best_of_two", [P, SLOTS * V], BF16)
-        for half in halves:
-            nc.vector.tensor_tensor(best_of_two[:, half], rounded[0][:, half], rounded[2][:, half], ALU.max)
-
         parts = [slice(0, HALF_V // 2), slice(HALF_V // 2, HALF_V)]
         pairs = [slice(0, SLOTS // 2), slice(SLOTS // 2, SLOTS)]
-        all_slots = [slice(0, SLOTS)]
         out_words = own_tile("out_words", [P, V], U32)
         out_scales = own_tile("out_scales", [P, V], U8)
         out_rows_hbm = out_0.rearrange("(p t) v -> p t v", t=SLOTS)
         out_words_hbm = out_1[0].rearrange("p v b -> p (v b)").bitcast(I32)
-        for h in range(2):
-            last_half = h == 1
-            states = columns[h]
-            z = own_tile("z%d" % h, [P, SLOTS * HALF_V], BF16)
-            second_here = rounded[1][:, halves[h]]
-            best_here = best_of_two[:, halves[h]]
-            for part in parts:
-                flat = woven(part)
-                nc.vector.tensor_tensor(z[:, flat], second_here[:, flat], best_here[:, flat], ALU.max)
-            z_words = own_tile("z_words%d" % h, [P, HALF_V], U32)
-            z_scales = own_tile("z_scales%d" % h, [P, HALF_V], U8)
-            for part in parts:
-                nc.vector.quantize_mx(z_words[:, part].bitcast(FP8X4), z_scales[:, part], z[:, woven(part)])
 
+        def add_third(name, states):
+            tile = own_tile(name, [P, SLOTS * (states.stop - states.start)], BF16)
+            nc.vector.tensor_tensor(
+                slots_together(tile[:]), slots_apart(third[:, :, states]), slots_apart(steps[2][:, :, states]), ALU.add
+            )
+            return tile
+
+        def larger(name, tile, l, states):
+            best = own_tile(name, [P, SLOTS * (states.stop - states.start)], BF16)
+            nc.vector.tensor_tensor(best[:], tile[:], rounded[l][:, woven(states)], ALU.max)
+            return best
+
+        z_words = [own_tile("z_words%d" % h, [P, HALF_V], U32) for h in range(2)]
+        z_scales = [own_tile("z_scales%d" % h, [P, HALF_V], U8) for h in range(2)]
+
+        def quantise(h, part, z):
+            nc.vector.quantize_mx(z_words[h][:, part].bitcast(FP8X4), z_scales[h][:, part], z[:])
+
+        quarters = [slice(HALF_V + part.start, HALF_V + part.stop) for part in parts]
+        sums_first = add_third("sums_a", columns[0])
+        sums_q0 = add_third("sums_b", quarters[0])
+        best_first = larger("best_a", sums_first, 0, columns[0])
+        sums_q1 = add_third("sums0", quarters[1])
+        z_first = larger("z_a", best_first, 1, columns[0])
+        best_q0 = larger("best_c", sums_q0, 0, quarters[0])
+        quantise(0, slice(0, HALF_V), z_first)
+        best_q1 = larger("best_b", sums_q1, 0, quarters[1])
+        z_q0 = larger("z_b", best_q0, 1, quarters[0])
+        z_q1 = larger("z_c", best_q1, 1, quarters[1])
+        quantise(1, parts[0], z_q0)
+        quantise(1, parts[1], z_q1)
+
+        results = []
+        for h in range(2):
+            states = columns[h]
             result = own_tile("result%d" % h, [P, SLOTS, HALF_V], F32)
             for g, pair in enumerate(pairs):
                 bank = psum.tile([P, SLOTS // 2, HALF_V], F32, name="bank%d" % (len(pairs) * h + g))
@@ -224,28 +234,43 @@ def tile_picked_tropic_relu_po_kernel(
                         bank[:, t - pair.start, :],
                         lhsT=w2_words_dealt[:, 2 * P * t : 2 * P * (t + 1)].bitcast(FP4X4),
                         lhsT_scale=w2_scales_placed[:, P * t : P * (t + 1)],
-                        rhs=z_words[:].bitcast(FP8X4),
-                        rhs_scale=z_scales[:],
+                        rhs=z_words[h][:].bitcast(FP8X4),
+                        rhs_scale=z_scales[h][:],
                         start=True,
                         stop=True,
                     )
                 nc.scalar.copy(result[:, pair, :], bank[:])
             nc.sync.dma_start(out_rows_hbm[:, :, states], result[:])
+            results.append(result)
 
-            result_rounded = own_tile("result_rounded%d" % h, [P, SLOTS * HALF_V], BF16)
-            for slots in pairs if last_half else all_slots:
-                for part in parts:
-                    nc.vector.tensor_copy(
-                        slots_together(result_rounded[:, woven(part)])[:, :, slots, :],
-                        slots_apart(result[:, slots, part]),
-                    )
-            for part in parts:
-                nc.vector.quantize_mx(
-                    out_words[:, states][:, part].bitcast(FP8X4),
-                    out_scales[:, states][:, part],
-                    result_rounded[:, woven(part)],
-                )
-            nc.sync.dma_start(out_words_hbm[:, states], out_words[:, states].bitcast(I32))
+        result_rounded = [own_tile("result_rounded%d" % h, [P, SLOTS * HALF_V], BF16) for h in range(2)]
+
+        def round_result(h, slots, part):
+            nc.vector.tensor_copy(
+                slots_together(result_rounded[h][:, woven(part)])[:, :, slots, :],
+                slots_apart(results[h][:, slots, part]),
+            )
+
+        def quantise_result(h, part):
+            nc.vector.quantize_mx(
+                out_words[:, columns[h]][:, part].bitcast(FP8X4),
+                out_scales[:, columns[h]][:, part],
+                result_rounded[h][:, woven(part)],
+            )
+
+        def store_words(h):
+            nc.sync.dma_start(out_words_hbm[:, columns[h]], out_words[:, columns[h]].bitcast(I32))
+
+        whole = slice(0, HALF_V)
+        round_result(0, slice(0, SLOTS), whole)
+        round_result(1, pairs[0], whole)
+        quantise_result(0, whole)
+        store_words(0)
+        for part in parts:
+            round_result(1, pairs[1], part)
+        for part in parts:
+            quantise_result(1, part)
+        store_words(1)
 
         for r in range(ROWS):
             queue = nc.sync if r < ROWS // 2 else nc.scalar

@@ -174,16 +174,26 @@ def tile_picked_tropic_relu_po_kernel(
         step_sums = [own_tile("sums%d" % l, [P, SLOTS, V], F32) for l in range(2)]
         for t in range(SLOTS):
             nc.scalar.activation(third[:, t, :], y[t][:].indirect(lists[2][:]), ACT.Copy)
+        columns = [slice(h * HALF_V, (h + 1) * HALF_V) for h in range(2)]
         for l in range(2):
             for t in range(SLOTS):
-                looked_up = y[t][:].indirect(lists[l][:])
-                nc.vector.tensor_tensor(step_sums[l][:, t, :], looked_up, steps[l][:, t, :], ALU.add)
-        columns = [slice(h * HALF_V, (h + 1) * HALF_V) for h in range(2)]
+                states = columns[0] if (l, t) == (1, SLOTS - 1) else slice(0, V)
+                looked_up = y[t][:].indirect(lists[l][:, : states.stop // PER_COLUMN])
+                nc.vector.tensor_tensor(step_sums[l][:, t, states], looked_up, steps[l][:, t, states], ALU.add)
         halves = [woven(c) for c in columns]
         rounded = [own_tile("sums_rounded%d" % l, [P, SLOTS * V], BF16) for l in range(2)]
-        nc.scalar.activation(slots_together(rounded[0][:]), slots_apart(step_sums[0][:]), ACT.Relu)
-        for h in range(2):
-            nc.scalar.copy(slots_together(rounded[1][:, halves[h]]), slots_apart(step_sums[1][:, :, columns[h]]))
+
+        def round_sums(l, h):
+            function = ACT.Relu if l == 0 else ACT.Copy
+            nc.scalar.activation(
+                slots_together(rounded[l][:, halves[h]]), slots_apart(step_sums[l][:, :, columns[h]]), function
+            )
+
+        second_rest = own_tile("second_rest", [P, HALF_V], F32)
+        nc.scalar.activation(second_rest[:], y[SLOTS - 1][:].indirect(lists[1][:, HALF_V // PER_COLUMN :]), ACT.Copy)
+        round_sums(0, 0)
+        round_sums(1, 0)
+        round_sums(0, 1)
         parts = [slice(0, HALF_V // 2), slice(HALF_V // 2, HALF_V)]
         pairs = [slice(0, SLOTS // 2), slice(SLOTS // 2, SLOTS)]
         out_words = own_tile("out_words", [P, V], U32)
@@ -211,12 +221,16 @@ def tile_picked_tropic_relu_po_kernel(
 
         quarters = [slice(HALF_V + part.start, HALF_V + part.stop) for part in parts]
         sums_first = add_third("sums_a", columns[0])
-        sums_q0 = add_third("sums_b", quarters[0])
+        nc.vector.tensor_tensor(
+            step_sums[1][:, SLOTS - 1, columns[1]], second_rest[:], steps[1][:, SLOTS - 1, columns[1]], ALU.add
+        )
+        round_sums(1, 1)
         best_first = larger("best_a", sums_first, 0, columns[0])
-        sums_q1 = add_third("sums0", quarters[1])
+        sums_q0 = add_third("sums_b", quarters[0])
         z_first = larger("z_a", best_first, 1, columns[0])
-        best_q0 = larger("best_c", sums_q0, 0, quarters[0])
+        sums_q1 = add_third("sums_c", quarters[1])
         quantise(0, slice(0, HALF_V), z_first)
+        best_q0 = larger("best_c", sums_q0, 0, quarters[0])
         best_q1 = larger("best_b", sums_q1, 0, quarters[1])
         z_q0 = larger("z_b", best_q0, 1, quarters[0])
         z_q1 = larger("z_c", best_q1, 1, quarters[1])

@@ -33,10 +33,10 @@ STEP_BYTES = 4 * SLOTS * V
 WORD_WINDOW = 0
 W1_ROUNDED = WORD_WINDOW + 4 * T
 STEP1 = W1_ROUNDED + 2 * SLOTS * H
-SCALE_WINDOW = STEP1 + STEP_BYTES - OVERLAP
-W2_WORDS = SCALE_WINDOW + OVERLAP
-STEP2 = SCALE_WINDOW + T - OVERLAP
-W1_RAW = STEP2 + STEP_BYTES
+W1_RAW = STEP1 + STEP_BYTES
+W2_WORDS = W1_RAW + OVERLAP
+STEP2 = W2_WORDS + 2 * N
+STEP3 = STEP2 + STEP_BYTES
 
 
 def slots_apart(ap):
@@ -80,13 +80,13 @@ def tile_picked_tropic_relu_po_kernel(
 
         picks = own_tile("picks", [P, S // PER_COLUMN], U16)
         lists = [own_tile("list%d" % l, [P, V // PER_COLUMN], U16) for l in range(3)]
-        x_scales_all = shared_tile("x_scales_all", [P, T], U8, SCALE_WINDOW)
+        x_scales_all = own_tile("x_scales_all", [P, T], U8)
         x_words_all = shared_tile("x_words_all", [P, T], U32, WORD_WINDOW)
         w1_raw = shared_tile("w1_raw", [P, SLOTS, H], F32, W1_RAW)
         w2_words_raw = shared_tile("w2_words_raw", [P, 2 * N], U8, W2_WORDS)
-        w2_scales_raw = own_tile("w2_scales_raw", [P, N], U8)
+        w2_scales_raw = shared_tile("w2_scales_raw", [P, N], U8, STEP1)
         steps = [
-            shared_tile("step%d" % l, [P, SLOTS, V], F32, offset) for l, offset in enumerate((STEP1, STEP2, W1_RAW))
+            shared_tile("step%d" % l, [P, SLOTS, V], F32, offset) for l, offset in enumerate((STEP1, STEP2, STEP3))
         ]
         x_scales_picked = own_tile("x_scales_picked", [P, S], U8)
 
@@ -107,18 +107,23 @@ def tile_picked_tropic_relu_po_kernel(
         x_scales_gathered = own_tile("x_scales_gathered", [P, S], U8)
         nc.vector.tensor_copy(x_scales_gathered[:], x_scales_all[:].indirect(picks[:]))
         for r in range(ROWS):
-            nc.sync.dma_start(placed_rows(x_scales_picked, r), loaded_rows(x_scales_gathered, r))
-        nc.sync.dma_start(w2_words_raw[:].bitcast(I32), w2_words[0].bitcast(I32))
+            nc.scalar.dma_start(placed_rows(x_scales_picked, r), loaded_rows(x_scales_gathered, r))
+
+        w2_scales_dealt = own_tile("w2_scales_dealt", [P, N], U8)
+        nc.vector.tensor_copy(
+            w2_scales_dealt[:].rearrange("p (t m) -> p t m", t=SLOTS),
+            w2_scales_raw[:].rearrange("p (m t) -> p t m", t=SLOTS),
+        )
         nc.sync.dma_start(steps[0][:], step_rows[0])
-        nc.sync.dma_start(steps[1][:], step_rows[1])
 
         w1_from = w1_raw[:].rearrange("p j (m t) -> p m j t", t=SLOTS)
         w1_words = own_tile("w1_words", [P, H], U32)
         w1_scales = own_tile("w1_scales", [P, H], U8)
         w1_rounded = shared_tile("w1_rounded", [P, SLOTS * H], BF16, W1_ROUNDED)
         w1_to = w1_rounded[:].rearrange("p (t m j) -> p m j t", t=SLOTS, j=SLOTS)
-        nc.scalar.copy(w1_to[:, :SCALAR_GROUPS], w1_from[:, :SCALAR_GROUPS])
-        nc.vector.tensor_copy(w1_to[:, SCALAR_GROUPS:], w1_from[:, SCALAR_GROUPS:])
+        nc.vector.tensor_copy(w1_to, w1_from)
+        nc.sync.dma_start(w2_words_raw[:].bitcast(I32), w2_words[0].bitcast(I32))
+        nc.sync.dma_start(steps[1][:], step_rows[1])
         nc.sync.dma_start(steps[2][:], step_rows[2])
 
         nc.vector.quantize_mx(w1_words[:].bitcast(FP8X4), w1_scales[:], w1_rounded[:])
@@ -156,16 +161,11 @@ def tile_picked_tropic_relu_po_kernel(
         first_product(3, slice(0, S), 6, nc.scalar.copy)
 
         w2_words_dealt = shared_tile("w2_words_dealt", [P, 2 * N], U8, WORD_WINDOW)
-        w2_scales_dealt = own_tile("w2_scales_dealt", [P, N], U8)
         w2_scales_placed = shared_tile("w2_scales_placed", [P, N], U8, WORD_WINDOW + 2 * N)
         nc.vector.memset(w2_scales_placed[:].bitcast(I32), 0)
         nc.vector.tensor_copy(
             w2_words_dealt[:].bitcast(U16).rearrange("p (t m) -> p t m", t=SLOTS),
             w2_words_raw[:].bitcast(U16).rearrange("p (m t) -> p t m", t=SLOTS),
-        )
-        nc.vector.tensor_copy(
-            w2_scales_dealt[:].rearrange("p (t m) -> p t m", t=SLOTS),
-            w2_scales_raw[:].rearrange("p (m t) -> p t m", t=SLOTS),
         )
         for r in range(ROWS):
             nc.sync.dma_start(placed_rows(w2_scales_placed, r), loaded_rows(w2_scales_dealt, r))

@@ -26,8 +26,6 @@ QUARTER_S = S // 4
 HALF_V = V // 2
 FLOPS = 2 * K * H * S + 2 * H * N * V
 
-SCALAR_GROUPS = 44
-
 OVERLAP = 64
 STEP_BYTES = 4 * SLOTS * V
 WORD_WINDOW = 0
@@ -170,72 +168,107 @@ def tile_picked_tropic_relu_po_kernel(
         for r in range(ROWS):
             nc.sync.dma_start(placed_rows(w2_scales_placed, r), loaded_rows(w2_scales_dealt, r))
 
-        third = own_tile("third", [P, SLOTS, V], F32)
-        step_sums = [own_tile("sums%d" % l, [P, SLOTS, V], F32) for l in range(2)]
-        for t in range(SLOTS):
-            nc.scalar.activation(third[:, t, :], y[t][:].indirect(lists[2][:]), ACT.Copy)
+        everything = slice(0, V)
         columns = [slice(h * HALF_V, (h + 1) * HALF_V) for h in range(2)]
-        for l in range(2):
-            for t in range(SLOTS):
-                states = columns[0] if (l, t) == (1, SLOTS - 1) else slice(0, V)
-                looked_up = y[t][:].indirect(lists[l][:, : states.stop // PER_COLUMN])
-                nc.vector.tensor_tensor(step_sums[l][:, t, states], looked_up, steps[l][:, t, states], ALU.add)
-        halves = [woven(c) for c in columns]
-        rounded = [own_tile("sums_rounded%d" % l, [P, SLOTS * V], BF16) for l in range(2)]
+        parts = [slice(0, HALF_V // 2), slice(HALF_V // 2, HALF_V)]
+        quarters = [slice(HALF_V + part.start, HALF_V + part.stop) for part in parts]
+        pairs = [slice(0, SLOTS // 2), slice(SLOTS // 2, SLOTS)]
+        sums = [own_tile("sums%d" % l, [P, SLOTS, V], F32) for l in range(2)]
+        second = own_tile("second", [P, 2, V], F32)
+        third = own_tile("third", [P, SLOTS, V], F32)
 
-        def round_sums(l, h):
-            function = ACT.Relu if l == 0 else ACT.Copy
-            nc.scalar.activation(
-                slots_together(rounded[l][:, halves[h]]), slots_apart(step_sums[l][:, :, columns[h]]), function
+        def fetch(into, l, t, states):
+            entries = lists[l][:, states.start // PER_COLUMN : states.stop // PER_COLUMN]
+            nc.scalar.activation(into[:, t, states], y[t][:].indirect(entries), ACT.Copy)
+
+        def fetch_and_add(l, t):
+            nc.vector.tensor_tensor(sums[l][:, t, :], y[t][:].indirect(lists[l][:]), steps[l][:, t, :], ALU.add)
+
+        for t in range(2):
+            fetch(second, 1, t, everything)
+        for t in range(2):
+            fetch(third, 2, t, everything)
+        for states in columns:
+            for t in range(2, SLOTS):
+                fetch(third, 2, t, states)
+        for t in range(SLOTS):
+            fetch_and_add(0, t)
+        for t in range(2, SLOTS):
+            fetch_and_add(1, t)
+
+        best12 = own_tile("best12", [P, SLOTS * V], BF16)
+        sums3 = own_tile("sums3", [P, SLOTS * V], BF16)
+        z = own_tile("z", [P, SLOTS * V], BF16)
+        z_words = [own_tile("z_words%d" % h, [P, HALF_V], U32) for h in range(2)]
+        z_scales = [own_tile("z_scales%d" % h, [P, HALF_V], U8) for h in range(2)]
+
+        def add_second(states):
+            nc.vector.tensor_tensor(
+                sums[1][:, pairs[0], states], second[:, :, states], steps[1][:, pairs[0], states], ALU.add
             )
 
-        second_rest = own_tile("second_rest", [P, HALF_V], F32)
-        nc.scalar.activation(second_rest[:], y[SLOTS - 1][:].indirect(lists[1][:, HALF_V // PER_COLUMN :]), ACT.Copy)
-        round_sums(0, 0)
-        round_sums(1, 0)
-        round_sums(0, 1)
-        parts = [slice(0, HALF_V // 2), slice(HALF_V // 2, HALF_V)]
-        pairs = [slice(0, SLOTS // 2), slice(SLOTS // 2, SLOTS)]
+        rounded = [own_tile("rounded%d" % l, [P, SLOTS * HALF_V], BF16) for l in range(2)]
+
+        def round_late(l):
+            function = ACT.Relu if l == 0 else ACT.Copy
+            nc.scalar.activation(slots_together(rounded[l][:]), slots_apart(sums[l][:, :, columns[1]]), function)
+
+        def late_larger(q):
+            nc.vector.tensor_tensor(
+                best12[:, woven(quarters[q])], sums3[:, woven(quarters[q])], rounded[0][:, woven(parts[q])], ALU.max
+            )
+
+        def late_largest(q):
+            nc.vector.tensor_tensor(
+                z[:, woven(quarters[q])], best12[:, woven(quarters[q])], rounded[1][:, woven(parts[q])], ALU.max
+            )
+
+        def larger12(states):
+            nc.vector.scalar_tensor_tensor(
+                best12[:, woven(states)].rearrange("p (v t) -> p v t", t=SLOTS),
+                sums[0][:, :, states].rearrange("p t v -> p v t"),
+                0.0,
+                sums[1][:, :, states].rearrange("p t v -> p v t"),
+                ALU.max,
+                ALU.max,
+            )
+
+        def add_third(states):
+            nc.vector.tensor_tensor(
+                slots_together(sums3[:, woven(states)]),
+                slots_apart(third[:, :, states]),
+                slots_apart(steps[2][:, :, states]),
+                ALU.add,
+            )
+
+        def largest(states):
+            nc.vector.tensor_tensor(z[:, woven(states)], best12[:, woven(states)], sums3[:, woven(states)], ALU.max)
+
+        def quantise(h, part):
+            states = slice(h * HALF_V + part.start, h * HALF_V + part.stop)
+            nc.vector.quantize_mx(z_words[h][:, part].bitcast(FP8X4), z_scales[h][:, part], z[:, woven(states)])
+
+        add_second(columns[0])
+        add_second(columns[1])
+        round_late(0)
+        round_late(1)
+        larger12(columns[0])
+        add_third(columns[0])
+        add_third(quarters[0])
+        largest(columns[0])
+        add_third(quarters[1])
+        quantise(0, slice(0, HALF_V))
+        late_larger(0)
+        late_larger(1)
+        late_largest(0)
+        late_largest(1)
+        quantise(1, parts[0])
+        quantise(1, parts[1])
+
         out_words = own_tile("out_words", [P, V], U32)
         out_scales = own_tile("out_scales", [P, V], U8)
         out_rows_hbm = out_0.rearrange("(p t) v -> p t v", t=SLOTS)
         out_words_hbm = out_1[0].rearrange("p v b -> p (v b)").bitcast(I32)
-
-        def add_third(name, states):
-            tile = own_tile(name, [P, SLOTS * (states.stop - states.start)], BF16)
-            nc.vector.tensor_tensor(
-                slots_together(tile[:]), slots_apart(third[:, :, states]), slots_apart(steps[2][:, :, states]), ALU.add
-            )
-            return tile
-
-        def larger(name, tile, l, states):
-            best = own_tile(name, [P, SLOTS * (states.stop - states.start)], BF16)
-            nc.vector.tensor_tensor(best[:], tile[:], rounded[l][:, woven(states)], ALU.max)
-            return best
-
-        z_words = [own_tile("z_words%d" % h, [P, HALF_V], U32) for h in range(2)]
-        z_scales = [own_tile("z_scales%d" % h, [P, HALF_V], U8) for h in range(2)]
-
-        def quantise(h, part, z):
-            nc.vector.quantize_mx(z_words[h][:, part].bitcast(FP8X4), z_scales[h][:, part], z[:])
-
-        quarters = [slice(HALF_V + part.start, HALF_V + part.stop) for part in parts]
-        sums_first = add_third("sums_a", columns[0])
-        nc.vector.tensor_tensor(
-            step_sums[1][:, SLOTS - 1, columns[1]], second_rest[:], steps[1][:, SLOTS - 1, columns[1]], ALU.add
-        )
-        round_sums(1, 1)
-        best_first = larger("best_a", sums_first, 0, columns[0])
-        sums_q0 = add_third("sums_b", quarters[0])
-        z_first = larger("z_a", best_first, 1, columns[0])
-        sums_q1 = add_third("sums_c", quarters[1])
-        quantise(0, slice(0, HALF_V), z_first)
-        best_q0 = larger("best_c", sums_q0, 0, quarters[0])
-        best_q1 = larger("best_b", sums_q1, 0, quarters[1])
-        z_q0 = larger("z_b", best_q0, 1, quarters[0])
-        z_q1 = larger("z_c", best_q1, 1, quarters[1])
-        quantise(1, parts[0], z_q0)
-        quantise(1, parts[1], z_q1)
 
         results = []
         for h in range(2):

@@ -155,8 +155,10 @@ def tile_picked_tropic_relu_po_kernel(
         first_product(0, slice(HALF_S, HALF_S + QUARTER_S), 2, nc.vector.tensor_copy)
         first_product(0, slice(HALF_S + QUARTER_S, S), 3, nc.scalar.copy)
         first_product(1, second_half, 4, nc.scalar.copy)
-        first_product(2, slice(0, S), 5, nc.scalar.copy)
-        first_product(3, slice(0, S), 6, nc.scalar.copy)
+        first_product(2, first_half, 5, nc.scalar.copy)
+        first_product(2, second_half, 6, nc.scalar.copy)
+        first_product(3, first_half, 7, nc.scalar.copy)
+        first_product(3, second_half, 0, nc.scalar.copy)
 
         w2_words_dealt = shared_tile("w2_words_dealt", [P, 2 * N], U8, WORD_WINDOW)
         w2_scales_placed = shared_tile("w2_scales_placed", [P, N], U8, WORD_WINDOW + 2 * N)

@@ -276,8 +276,9 @@ def tile_picked_tropic_relu_po_kernel(
         for h in range(2):
             states = columns[h]
             result = own_tile("result%d" % h, [P, SLOTS, HALF_V], F32)
-            for g, pair in enumerate(pairs):
-                bank = psum.tile([P, SLOTS // 2, HALF_V], F32, name="bank%d" % (len(pairs) * h + g))
+            groups = [slice(t, t + 1) for t in range(SLOTS)]
+            for g, pair in enumerate(groups):
+                bank = psum.tile([P, pair.stop - pair.start, HALF_V], F32, name="bank%d" % (SLOTS * h + g))
                 for t in range(pair.start, pair.stop):
                     nc.tensor.matmul_mx(
                         bank[:, t - pair.start, :],

@@ -26,7 +26,7 @@ QUARTER_S = S // 4
 HALF_V = V // 2
 FLOPS = 2 * K * H * S + 2 * H * N * V
 
-OVERLAP = 64
+OVERLAP = 256
 STEP_BYTES = 4 * SLOTS * V
 WORD_WINDOW = 0
 W1_ROUNDED = WORD_WINDOW + 4 * T
@@ -71,10 +71,10 @@ def tile_picked_tropic_relu_po_kernel(
         psum = ctx.enter_context(tc.psum_pool(name="psum", bufs=1))
 
         def own_tile(name, shape, dtype):
-            return held.tile(shape, dtype, name=name, align_bytes=64)
+            return held.tile(shape, dtype, name=name, align_bytes=256)
 
         def shared_tile(name, shape, dtype, offset):
-            return shared.tile(shape, dtype, name=name, offset=offset, align_bytes=64)
+            return shared.tile(shape, dtype, name=name, offset=offset, align_bytes=256)
 
         picks = own_tile("picks", [P, S // PER_COLUMN], U16)
         lists = [own_tile("list%d" % l, [P, V // PER_COLUMN], U16) for l in range(3)]

@@ -21,6 +21,7 @@ PER_COLUMN = 16
 K, T, S, V, N, H = 512, 2048, 512, 256, 512, 512
 ALL_ROWS = ROWS * P // QUADRANT
 ROWS_AT = P - ALL_ROWS
+SPREAD_AT = QUADRANT
 HALF_S = S // 2
 QUARTER_S = S // 4
 HALF_V = V // 2
@@ -55,6 +56,10 @@ def placed_rows(tile, r):
 
 def loaded_rows(tile, r):
     return tile[ROWS_AT + r : P : ROWS, :].bitcast(I32)
+
+
+def spread_rows(tile, r):
+    return tile[SPREAD_AT + ROWS * r : SPREAD_AT + ROWS * ALL_ROWS : ROWS * ROWS, :].bitcast(I32)
 
 
 def hbm_rows(scales, r):
@@ -126,6 +131,7 @@ def tile_picked_tropic_relu_po_kernel(
 
         nc.vector.quantize_mx(w1_words[:].bitcast(FP8X4), w1_scales[:], w1_rounded[:])
 
+
         x_words_picked = shared_tile("x_words_picked", [P, S], U32, W1_ROUNDED)
         y = [own_tile("y%d" % t, [P, S], F32) for t in range(SLOTS)]
 
@@ -169,6 +175,7 @@ def tile_picked_tropic_relu_po_kernel(
         )
         for r in range(ROWS):
             nc.sync.dma_start(placed_rows(w2_scales_placed, r), loaded_rows(w2_scales_dealt, r))
+
 
         everything = slice(0, V)
         columns = [slice(h * HALF_V, (h + 1) * HALF_V) for h in range(2)]
@@ -267,6 +274,7 @@ def tile_picked_tropic_relu_po_kernel(
         quantise(1, parts[0])
         quantise(1, parts[1])
 
+
         out_words = own_tile("out_words", [P, V], U32)
         out_scales = own_tile("out_scales", [P, V], U8)
         out_rows_hbm = out_0.rearrange("(p t) v -> p t v", t=SLOTS)
@@ -289,8 +297,11 @@ def tile_picked_tropic_relu_po_kernel(
                         start=True,
                         stop=True,
                     )
-                nc.scalar.copy(result[:, pair, :], bank[:])
-            nc.sync.dma_start(out_rows_hbm[:, :, states], result[:])
+                last = h == 1 and g == SLOTS - 1
+                for part in parts if last else [slice(0, HALF_V)]:
+                    nc.scalar.copy(result[:, pair, part], bank[:, :, part])
+            for slots in pairs:
+                nc.sync.dma_start(out_rows_hbm[:, slots, states], result[:, slots, :])
             results.append(result)
 
         result_rounded = [own_tile("result_rounded%d" % h, [P, SLOTS * HALF_V], BF16) for h in range(2)]
@@ -313,9 +324,9 @@ def tile_picked_tropic_relu_po_kernel(
 
         whole = slice(0, HALF_V)
         round_result(0, slice(0, SLOTS), whole)
-        round_result(1, pairs[0], whole)
         quantise_result(0, whole)
         store_words(0)
+        round_result(1, pairs[0], whole)
         for part in parts:
             round_result(1, pairs[1], part)
         for part in parts:

from contextlib import ExitStack

import concourse.mybir as mybir

F32 = mybir.dt.float32
BF16 = mybir.dt.bfloat16
I32 = mybir.dt.int32
U32 = mybir.dt.uint32
U16 = mybir.dt.uint16
U8 = mybir.dt.uint8
FP8X4 = mybir.dt.float8_e4m3fn_x4
FP4X4 = mybir.dt.float4_e2m1fn_x4
ALU = mybir.AluOpType
ACT = mybir.ActivationFunctionType

P = 128
SLOTS = 4
QUADRANT = 32
ROWS = 4
PER_COLUMN = 16
K, T, S, V, N, H = 512, 2048, 512, 256, 512, 512
ALL_ROWS = ROWS * P // QUADRANT
ROWS_AT = P - ALL_ROWS
SPREAD_AT = QUADRANT
HALF_S = S // 2
QUARTER_S = S // 4
HALF_V = V // 2
FLOPS = 2 * K * H * S + 2 * H * N * V

OVERLAP = 256
STEP_BYTES = 4 * SLOTS * V
WORD_WINDOW = 0
W1_ROUNDED = WORD_WINDOW + 4 * T
STEP1 = W1_ROUNDED + 2 * SLOTS * H
W1_RAW = STEP1 + STEP_BYTES
W2_WORDS = W1_RAW + OVERLAP
STEP2 = W2_WORDS + 2 * N
STEP3 = STEP2 + STEP_BYTES


def slots_apart(ap):
    return ap.rearrange("p t (c e) -> p c t e", e=4)


def slots_together(ap):
    return ap.rearrange("p (c e t) -> p c t e", e=4, t=SLOTS)


def woven(columns):
    return slice(SLOTS * columns.start, SLOTS * columns.stop)


def placed_rows(tile, r):
    return tile[r:P:QUADRANT, :].bitcast(I32)


def loaded_rows(tile, r):
    return tile[ROWS_AT + r : P : ROWS, :].bitcast(I32)


def spread_rows(tile, r):
    return tile[SPREAD_AT + ROWS * r : SPREAD_AT + ROWS * ALL_ROWS : ROWS * ROWS, :].bitcast(I32)


def hbm_rows(scales, r):
    return scales[0, r:ALL_ROWS:ROWS, :].bitcast(I32)


def tile_picked_tropic_relu_po_kernel(
    tc, x_words, x_scales, w1, t1, t2, t3, w2_words, w2_scales, offs, p1, p2, p3, out_0, out_1, out_2
):
    nc = tc.nc
    with ExitStack() as ctx:
        held = ctx.enter_context(tc.tile_pool(name="held", bufs=1))
        shared = ctx.enter_context(tc.tile_pool(name="shared", bufs=1))
        psum = ctx.enter_context(tc.psum_pool(name="psum", bufs=1))

        def own_tile(name, shape, dtype):
            return held.tile(shape, dtype, name=name, align_bytes=256)

        def shared_tile(name, shape, dtype, offset):
            return shared.tile(shape, dtype, name=name, offset=offset, align_bytes=256)

        picks = own_tile("picks", [P, S // PER_COLUMN], U16)
        lists = [own_tile("list%d" % l, [P, V // PER_COLUMN], U16) for l in range(3)]
        x_scales_all = own_tile("x_scales_all", [P, T], U8)
        x_words_all = shared_tile("x_words_all", [P, T], U32, WORD_WINDOW)
        w1_raw = shared_tile("w1_raw", [P, SLOTS, H], F32, W1_RAW)
        w2_words_raw = shared_tile("w2_words_raw", [P, 2 * N], U8, W2_WORDS)
        w2_scales_raw = shared_tile("w2_scales_raw", [P, N], U8, STEP1)
        steps = [
            shared_tile("step%d" % l, [P, SLOTS, V], F32, offset) for l, offset in enumerate((STEP1, STEP2, STEP3))
        ]
        x_scales_picked = own_tile("x_scales_picked", [P, S], U8)

        nc.vector.memset(x_scales_all[:ROWS_AT, :].bitcast(I32), 0)
        nc.vector.memset(w2_scales_raw[:ROWS_AT, :].bitcast(I32), 0)
        nc.vector.memset(x_scales_picked[:].bitcast(I32), 0)

        step_rows = [t.rearrange("(p t) v -> p t v", t=SLOTS) for t in (t1, t2, t3)]
        nc.sync.dma_start(picks[:], offs)
        nc.scalar.dma_start(x_scales_all[ROWS_AT:, :].bitcast(I32), x_scales[0].bitcast(I32))
        nc.scalar.dma_start(w2_scales_raw[ROWS_AT:, :].bitcast(I32), w2_scales[0].bitcast(I32))
        nc.sync.dma_start(w1_raw[:], w1.rearrange("(p j) c -> p j c", j=SLOTS))
        nc.sync.dma_start(lists[0][:], p1)
        nc.sync.dma_start(lists[1][:], p2)
        nc.sync.dma_start(x_words_all[:].bitcast(I32), x_words[0].rearrange("p n t -> p (n t)").bitcast(I32))
        nc.sync.dma_start(lists[2][:], p3)

        x_scales_gathered = own_tile("x_scales_gathered", [P, S], U8)
        nc.vector.tensor_copy(x_scales_gathered[:], x_scales_all[:].indirect(picks[:]))
        for r in range(ROWS):
            nc.scalar.dma_start(placed_rows(x_scales_picked, r), loaded_rows(x_scales_gathered, r))

        w2_scales_dealt = own_tile("w2_scales_dealt", [P, N], U8)
        nc.vector.tensor_copy(
            w2_scales_dealt[:].rearrange("p (t m) -> p t m", t=SLOTS),
            w2_scales_raw[:].rearrange("p (m t) -> p t m", t=SLOTS),
        )
        nc.sync.dma_start(steps[0][:], step_rows[0])

        w1_from = w1_raw[:].rearrange("p j (m t) -> p m j t", t=SLOTS)
        w1_words = own_tile("w1_words", [P, H], U32)
        w1_scales = own_tile("w1_scales", [P, H], U8)
        w1_rounded = shared_tile("w1_rounded", [P, SLOTS * H], BF16, W1_ROUNDED)
        w1_to = w1_rounded[:].rearrange("p (t m j) -> p m j t", t=SLOTS, j=SLOTS)
        nc.vector.tensor_copy(w1_to, w1_from)
        nc.sync.dma_start(w2_words_raw[:].bitcast(I32), w2_words[0].bitcast(I32))
        nc.sync.dma_start(steps[1][:], step_rows[1])
        nc.sync.dma_start(steps[2][:], step_rows[2])

        nc.vector.quantize_mx(w1_words[:].bitcast(FP8X4), w1_scales[:], w1_rounded[:])


        x_words_picked = shared_tile("x_words_picked", [P, S], U32, W1_ROUNDED)
        y = [own_tile("y%d" % t, [P, S], F32) for t in range(SLOTS)]

        def first_product(t, tokens, bank_number, copy_out):
            features = slice(t * P, (t + 1) * P)
            bank = psum.tile([P, tokens.stop - tokens.start], F32, name="bank%d" % bank_number)
            nc.tensor.matmul_mx(
                bank[:],
                lhsT=w1_words[:, features].bitcast(FP8X4),
                lhsT_scale=w1_scales[:, features],
                rhs=x_words_picked[:, tokens].bitcast(FP8X4),
                rhs_scale=x_scales_picked[:, tokens],
                start=True,
                stop=True,
            )
            copy_out(y[t][:, tokens], bank[:])

        def gather_words(tokens):
            entries = picks[:, tokens.start // PER_COLUMN : tokens.stop // PER_COLUMN]
            nc.vector.tensor_copy(x_words_picked[:, tokens], x_words_all[:].indirect(entries))

        first_half, second_half = slice(0, HALF_S), slice(HALF_S, S)
        gather_words(first_half)
        first_product(0, first_half, 0, nc.scalar.copy)
        first_product(1, first_half, 1, nc.scalar.copy)
        gather_words(second_half)
        first_product(0, slice(HALF_S, HALF_S + QUARTER_S), 2, nc.vector.tensor_copy)
        first_product(0, slice(HALF_S + QUARTER_S, S), 3, nc.scalar.copy)
        first_product(1, second_half, 4, nc.scalar.copy)
        first_product(2, first_half, 5, nc.scalar.copy)
        first_product(2, second_half, 6, nc.scalar.copy)
        first_product(3, first_half, 7, nc.scalar.copy)
        first_product(3, second_half, 0, nc.scalar.copy)

        w2_words_dealt = shared_tile("w2_words_dealt", [P, 2 * N], U8, WORD_WINDOW)
        w2_scales_placed = shared_tile("w2_scales_placed", [P, N], U8, WORD_WINDOW + 2 * N)
        nc.vector.memset(w2_scales_placed[:].bitcast(I32), 0)
        nc.vector.tensor_copy(
            w2_words_dealt[:].bitcast(U16).rearrange("p (t m) -> p t m", t=SLOTS),
            w2_words_raw[:].bitcast(U16).rearrange("p (m t) -> p t m", t=SLOTS),
        )
        for r in range(ROWS):
            nc.sync.dma_start(placed_rows(w2_scales_placed, r), loaded_rows(w2_scales_dealt, r))


        everything = slice(0, V)
        columns = [slice(h * HALF_V, (h + 1) * HALF_V) for h in range(2)]
        parts = [slice(0, HALF_V // 2), slice(HALF_V // 2, HALF_V)]
        quarters = [slice(HALF_V + part.start, HALF_V + part.stop) for part in parts]
        pairs = [slice(0, SLOTS // 2), slice(SLOTS // 2, SLOTS)]
        sums = [own_tile("sums%d" % l, [P, SLOTS, V], F32) for l in range(2)]
        second = own_tile("second", [P, 2, V], F32)
        third = own_tile("third", [P, SLOTS, V], F32)

        def fetch(into, l, t, states):
            entries = lists[l][:, states.start // PER_COLUMN : states.stop // PER_COLUMN]
            nc.scalar.activation(into[:, t, states], y[t][:].indirect(entries), ACT.Copy)

        def fetch_and_add(l, t):
            nc.vector.tensor_tensor(sums[l][:, t, :], y[t][:].indirect(lists[l][:]), steps[l][:, t, :], ALU.add)

        for t in range(2):
            fetch(second, 1, t, everything)
        for t in range(2):
            fetch(third, 2, t, everything)
        for states in columns:
            for t in range(2, SLOTS):
                fetch(third, 2, t, states)
        for t in range(SLOTS):
            fetch_and_add(0, t)
        for t in range(2, SLOTS):
            fetch_and_add(1, t)

        best12 = own_tile("best12", [P, SLOTS * V], BF16)
        sums3 = own_tile("sums3", [P, SLOTS * V], BF16)
        z = own_tile("z", [P, SLOTS * V], BF16)
        z_words = [own_tile("z_words%d" % h, [P, HALF_V], U32) for h in range(2)]
        z_scales = [own_tile("z_scales%d" % h, [P, HALF_V], U8) for h in range(2)]

        def add_second(states):
            nc.vector.tensor_tensor(
                sums[1][:, pairs[0], states], second[:, :, states], steps[1][:, pairs[0], states], ALU.add
            )

        rounded = [own_tile("rounded%d" % l, [P, SLOTS * HALF_V], BF16) for l in range(2)]

        def round_late(l):
            function = ACT.Relu if l == 0 else ACT.Copy
            nc.scalar.activation(slots_together(rounded[l][:]), slots_apart(sums[l][:, :, columns[1]]), function)

        def late_larger(q):
            nc.vector.tensor_tensor(
                best12[:, woven(quarters[q])], sums3[:, woven(quarters[q])], rounded[0][:, woven(parts[q])], ALU.max
            )

        def late_largest(q):
            nc.vector.tensor_tensor(
                z[:, woven(quarters[q])], best12[:, woven(quarters[q])], rounded[1][:, woven(parts[q])], ALU.max
            )

        def larger12(states):
            nc.vector.scalar_tensor_tensor(
                best12[:, woven(states)].rearrange("p (v t) -> p v t", t=SLOTS),
                sums[0][:, :, states].rearrange("p t v -> p v t"),
                0.0,
                sums[1][:, :, states].rearrange("p t v -> p v t"),
                ALU.max,
                ALU.max,
            )

        def add_third(states):
            nc.vector.tensor_tensor(
                slots_together(sums3[:, woven(states)]),
                slots_apart(third[:, :, states]),
                slots_apart(steps[2][:, :, states]),
                ALU.add,
            )

        def largest(states):
            nc.vector.tensor_tensor(z[:, woven(states)], best12[:, woven(states)], sums3[:, woven(states)], ALU.max)

        def quantise(h, part):
            states = slice(h * HALF_V + part.start, h * HALF_V + part.stop)
            nc.vector.quantize_mx(z_words[h][:, part].bitcast(FP8X4), z_scales[h][:, part], z[:, woven(states)])

        add_second(columns[0])
        add_second(columns[1])
        round_late(0)
        round_late(1)
        larger12(columns[0])
        add_third(columns[0])
        add_third(quarters[0])
        largest(columns[0])
        add_third(quarters[1])
        quantise(0, slice(0, HALF_V))
        late_larger(0)
        late_larger(1)
        late_largest(0)
        late_largest(1)
        quantise(1, parts[0])
        quantise(1, parts[1])


        out_words = own_tile("out_words", [P, V], U32)
        out_scales = own_tile("out_scales", [P, V], U8)
        out_rows_hbm = out_0.rearrange("(p t) v -> p t v", t=SLOTS)
        out_words_hbm = out_1[0].rearrange("p v b -> p (v b)").bitcast(I32)

        results = []
        for h in range(2):
            states = columns[h]
            result = own_tile("result%d" % h, [P, SLOTS, HALF_V], F32)
            groups = [slice(t, t + 1) for t in range(SLOTS)]
            for g, pair in enumerate(groups):
                bank = psum.tile([P, pair.stop - pair.start, HALF_V], F32, name="bank%d" % (SLOTS * h + g))
                for t in range(pair.start, pair.stop):
                    nc.tensor.matmul_mx(
                        bank[:, t - pair.start, :],
                        lhsT=w2_words_dealt[:, 2 * P * t : 2 * P * (t + 1)].bitcast(FP4X4),
                        lhsT_scale=w2_scales_placed[:, P * t : P * (t + 1)],
                        rhs=z_words[h][:].bitcast(FP8X4),
                        rhs_scale=z_scales[h][:],
                        start=True,
                        stop=True,
                    )
                last = h == 1 and g == SLOTS - 1
                for part in parts if last else [slice(0, HALF_V)]:
                    nc.scalar.copy(result[:, pair, part], bank[:, :, part])
            for slots in pairs:
                nc.sync.dma_start(out_rows_hbm[:, slots, states], result[:, slots, :])
            results.append(result)

        result_rounded = [own_tile("result_rounded%d" % h, [P, SLOTS * HALF_V], BF16) for h in range(2)]

        def round_result(h, slots, part):
            nc.vector.tensor_copy(
                slots_together(result_rounded[h][:, woven(part)])[:, :, slots, :],
                slots_apart(results[h][:, slots, part]),
            )

        def quantise_result(h, part):
            nc.vector.quantize_mx(
                out_words[:, columns[h]][:, part].bitcast(FP8X4),
                out_scales[:, columns[h]][:, part],
                result_rounded[h][:, woven(part)],
            )

        def store_words(h):
            nc.sync.dma_start(out_words_hbm[:, columns[h]], out_words[:, columns[h]].bitcast(I32))

        whole = slice(0, HALF_V)
        round_result(0, slice(0, SLOTS), whole)
        quantise_result(0, whole)
        store_words(0)
        round_result(1, pairs[0], whole)
        for part in parts:
            round_result(1, pairs[1], part)
        for part in parts:
            quantise_result(1, part)
        store_words(1)

        for r in range(ROWS):
            queue = nc.sync if r < ROWS // 2 else nc.scalar
            queue.dma_start(hbm_rows(out_2, r), placed_rows(out_scales, r))
